import numpy as np
import ml_dtypes


def mxq(x, axis, fmt="e4m3"):
    dtype, down = {"e4m3": (ml_dtypes.float8_e4m3fn, 7), "e5m2": (ml_dtypes.float8_e5m2, 14)}[fmt]
    v = np.moveaxis(np.asarray(x, np.float32).astype(ml_dtypes.bfloat16).astype(np.float64), axis, -1)
    blocks = v.reshape(v.shape[:-1] + (-1, 32))
    amax = np.abs(blocks).max(-1, keepdims=True)
    byte = np.maximum(np.where(amax > 0, np.frexp(amax)[1] - 1 + 127, 0) - down, 1)
    scale = np.exp2(byte - 127.0)
    codes = (blocks / scale).astype(np.float32).astype(dtype).astype(np.float64)
    return np.moveaxis((codes * scale).reshape(v.shape), -1, axis)


WIDE = False


def mx_kscale(k):
    if not WIDE:
        return np.ones(k)
    levels = np.array([10, -10, 5, -5, 0])
    if k % 512:
        return np.exp2(np.random.permutation(np.resize(levels, k // 32))).repeat(32)
    a = np.empty((k // 512, 16))
    for p in range(k // 512):
        a[p, :8] = np.random.permutation(np.resize(levels, 8))
        for g in range(8):
            far = levels[np.abs(levels - a[p, g]) >= 10]
            a[p, g + 8] = far[np.random.randint(len(far))]
    return np.exp2(a.ravel()).repeat(32)


def f64(x):
    return np.asarray(x).astype(np.float64)


def striped(idx):
    return np.tile(idx.reshape(-1, 16).T, (8, 1)).astype(np.uint16)


def unstriped(offs):
    return offs[:16].T.reshape(-1).astype(np.int64)


E2M1 = np.array([0.0, 0.5, 1.0, 1.5, 2.0, 3.0, 4.0, 6.0, -0.0, -0.5, -1.0, -1.5, -2.0, -3.0, -4.0, -6.0])


def pack_weight(w, fmt):
    k, n = w.shape
    w = f64(np.asarray(w, np.float32).astype(ml_dtypes.bfloat16)).reshape(k // 32, 32, n)
    amax = np.abs(w).max(1)
    if fmt == "e4m3":
        byte = np.frexp(amax)[1] - 1 + 127 - 7
    else:
        mant, ex = np.frexp(amax / 6.0)
        byte = np.where(mant > 0.5, ex, ex - 1) + 127
    byte = np.clip(np.where(amax > 0, byte, 1), 1, 254)
    scaled = (w * np.exp2(127.0 - byte)[:, None, :]).reshape(k, n).astype(np.float32)
    by_word = np.ascontiguousarray(scaled.reshape(k // 512, 128, 4, n).transpose(0, 1, 3, 2))
    if fmt == "e4m3":
        words = by_word.astype(ml_dtypes.float8_e4m3fn).view(np.uint8)
    else:
        c = by_word.astype(ml_dtypes.float4_e2m1fn).view(np.uint8) & 0xF
        words = (c[..., 0::2] | (c[..., 1::2] << 4)).reshape(k // 512, 128, 2 * n)
    return np.ascontiguousarray(words), np.ascontiguousarray(byte.astype(np.uint8).reshape(k // 512, 16, n))


def unpack_weight(words, scales, fmt):
    g, _, n = scales.shape
    words = np.ascontiguousarray(words).reshape(g, 128, n, -1)
    if fmt == "e4m3":
        vals = words.view(ml_dtypes.float8_e4m3fn).astype(np.float64)
    else:
        nib = np.empty((g, 128, n, 4), np.uint8)
        nib[..., 0::2] = words & 0xF
        nib[..., 1::2] = words >> 4
        vals = E2M1[nib]
    vals = vals * np.repeat(np.exp2(scales.astype(np.float64) - 127.0), 8, axis=1)[..., None]
    return vals.transpose(0, 1, 3, 2).reshape(g * 512, n)


def gelu(v):
    return 0.5 * v * (1.0 + np.tanh(np.sqrt(2.0 / np.pi) * (v + 0.044715 * v**3)))


K, R, N, T, S, G = 2048, 512, 768, 2048, 1024, 16

def setup_inputs():
    n = np.random.standard_normal
    s = mx_kscale(K)[:, None]
    u = mx_kscale(R)[:, None]
    tab_words, tab_scales = pack_weight(n((K, T)) * s, "e4m3")
    wd_words, wd_scales = pack_weight(n((K, N)) / np.sqrt(K) / s, "e2m1")
    wa = n((K, R)) / np.sqrt(K) / s * u.T
    wb = 0.7 * n((R, N)) / np.sqrt(R) / u
    tenant = np.random.randint(0, G, S)
    gain = np.exp(0.3 * n((R, G)))[:, tenant]
    return {"tab_words": tab_words, "tab_scales": tab_scales,
            "offs": striped(np.random.permutation(T)[:S]),
            "wd_words": wd_words, "wd_scales": wd_scales,
            "wa": wa.astype(np.float32), "wb": wb.astype(np.float32),
            "gain": gain.astype(np.float32),
            "bq": (0.5 * n(N)).astype(np.float32)}

def reference(tab_words, tab_scales, offs, wd_words, wd_scales, wa, wb, gain, bq):
    v = unpack_weight(tab_words, tab_scales, "e4m3")[:, unstriped(offs)]
    wd = unpack_weight(wd_words, wd_scales, "e2m1")
    waq = mxq(f64(wa), 0, "e4m3")
    wbq = mxq(f64(wb), 0, "e4m3")
    h = (waq.T @ v) * f64(gain)
    hq = mxq(h, 0, "e4m3")
    y = wd.T @ v + wbq.T @ hq
    return y + f64(bq)[:, None]

@@ -1,0 +1,205 @@
+from contextlib import ExitStack
+
+import concourse.mybir as mybir
+
+K, R, N, T, S = 2048, 512, 768, 2048, 1024
+FLOPS = 2 * S * (K * R + K * N + R * N)
+
+F32 = mybir.dt.float32
+BF16 = mybir.dt.bfloat16
+I32 = mybir.dt.int32
+U32 = mybir.dt.uint32
+U16 = mybir.dt.uint16
+U8 = mybir.dt.uint8
+FP8X4 = mybir.dt.float8_e4m3fn_x4
+FP4X4 = mybir.dt.float4_e2m1fn_x4
+COPY = mybir.ActivationFunctionType.Copy
+IDENTITY = mybir.ActivationFunctionType.Identity
+MULT = mybir.AluOpType.mult
+
+P = 128
+PACK = 4
+PASSES = K // (P * PACK)
+HALF = 512
+HALVES = S // HALF
+N_TILES = N // P
+QUADS = 4
+BANKS = 8
+SHIFT_ROWS = 112
+
+
+def tile_list_tenant_adapter_queries_kernel(
+    tc, tab_words, tab_scales, offs, wd_words, wd_scales, wa, wb, gain, bq, out
+):
+    nc = tc.nc
+    with ExitStack() as ctx:
+        keep = ctx.enter_context(tc.tile_pool(name="keep", bufs=1))
+        stage = ctx.enter_context(tc.tile_pool(name="stage", bufs=12))
+        psum = ctx.enter_context(tc.psum_pool(name="psum", bufs=1))
+
+        def held(shape, dtype, name):
+            return keep.tile(shape, dtype, name=name, align_bytes=64)
+
+        def bank(b):
+            return psum.tile([P, HALF], F32, name="bank%d" % b)
+
+        offsets = keep.tile([P, S // 16], U16, name="offsets")
+        nc.sync.dma_start(offsets[:], offs)
+
+        tab_sc = held([P, T], U8, "tab_sc")
+        wd_sc = held([P, PASSES, N], U8, "wd_sc")
+        v_sc_low = held([P, PASSES - 1, S], U8, "v_sc_low")
+        nc.gpsimd.memset(tab_sc[:].bitcast(I32), 0)
+        nc.vector.memset(wd_sc[:].bitcast(I32), 0)
+        nc.vector.memset(v_sc_low[:].bitcast(I32), 0)
+        for q in range(QUADS):
+            nc.sync.dma_start(
+                out=tab_sc[32 * q : 32 * q + 16, :].bitcast(I32),
+                in_=tab_scales[:, 4 * q : 4 * q + 4, :].bitcast(I32),
+            )
+        for q in range(QUADS):
+            nc.gpsimd.dma_start(
+                out=wd_sc[32 * q : 32 * q + 4, :, :].bitcast(I32),
+                in_=wd_scales[:, 4 * q : 4 * q + 4, :].rearrange("a r n -> r a n").bitcast(I32),
+            )
+
+        v_sc = held([P, S], U8, "v_sc")
+        nc.vector.tensor_copy(out=v_sc[:], in_=tab_sc[:].indirect(offsets[:]))
+
+        def shift_scales(s):
+            for a in range(1, PASSES):
+                nc.sync.dma_start(
+                    out=v_sc_low[0:SHIFT_ROWS, a - 1, s * HALF : (s + 1) * HALF].bitcast(I32),
+                    in_=v_sc[4 * a : 4 * a + SHIFT_ROWS, s * HALF : (s + 1) * HALF].bitcast(I32),
+                )
+
+        wa_raw, tab = [], []
+        for a in range(PASSES):
+            wa_raw.append(held([P, PACK, R], F32, "wa_raw%d" % a))
+            nc.sync.dma_start(
+                out=wa_raw[a][:],
+                in_=wa[a * P * PACK : (a + 1) * P * PACK, :].rearrange("(p j) c -> p j c", j=PACK),
+            )
+            tab.append(held([P, T], I32, "tab%d" % a))
+            nc.sync.dma_start(out=tab[a][:], in_=tab_words[a].rearrange("p t i -> p (t i)").bitcast(I32))
+        wd = held([P, PASSES, 2 * N], U8, "wd")
+        nc.sync.dma_start(out=wd[:].bitcast(I32), in_=wd_words.rearrange("a p c -> p a c").bitcast(I32))
+        shift_scales(0)
+        wb_raw = held([P, PACK, N], F32, "wb_raw")
+        nc.sync.dma_start(out=wb_raw[:], in_=wb.rearrange("(p j) n -> p j n", j=PACK))
+        gains = []
+        bias = held([P, N_TILES], F32, "bias")
+        for s in range(HALVES):
+            gains.append(held([P, PACK, HALF], F32, "gain%d" % s))
+            nc.sync.dma_start(
+                out=gains[s][:],
+                in_=gain[:, s * HALF : (s + 1) * HALF].rearrange("(p j) s -> p j s", j=PACK),
+            )
+            if s == 0:
+                shift_scales(1)
+                with nc.allow_non_contiguous_dma(reason="one bias value a partition"):
+                    nc.sync.dma_start(out=bias[:], in_=bq.rearrange("(c p) -> p c", p=P))
+
+
+        h_banks = [bank(b) for b in range(BANKS)]
+        v = [[None] * HALVES for a in range(PASSES)]
+        for a in range(PASSES):
+            grouped = held([P, PACK, P, PACK], BF16, "wa_grouped%d" % a)
+            dst = grouped[:].rearrange("p t m j -> p m j t")
+            src = wa_raw[a][:].rearrange("p j (m t) -> p m j t", t=PACK)
+            if a < PASSES - 1:
+                nc.scalar.activation(out=dst, in_=src, func=COPY)
+            else:
+                nc.scalar.activation(out=dst[:, : P // 2], in_=src[:, : P // 2], func=COPY)
+                nc.vector.tensor_copy(out=dst[:, P // 2 :], in_=src[:, P // 2 :])
+            wa_q = held([P, R], U32, "wa_q%d" % a)
+            wa_sc = held([P, R], U8, "wa_sc%d" % a)
+            nc.vector.quantize_mx(
+                out=wa_q[:].bitcast(FP8X4), scales=wa_sc[:], in_=grouped[:].rearrange("p t m j -> p (t m j)")
+            )
+            for s in range(HALVES):
+                v[a][s] = held([P, HALF], U32, "v%d_%d" % (a, s))
+                nc.vector.tensor_copy(
+                    out=v[a][s][:],
+                    in_=tab[a][:].bitcast(U32).indirect(offsets[:, s * HALF // 16 : (s + 1) * HALF // 16]),
+                )
+                for t in range(PACK):
+                    nc.tensor.matmul_mx(
+                        out=h_banks[PACK * s + t][:],
+                        lhsT=wa_q[:, t * P : (t + 1) * P].bitcast(FP8X4),
+                        lhsT_scale=wa_sc[:, t * P : (t + 1) * P],
+                        rhs=v[a][s][:].bitcast(FP8X4),
+                        rhs_scale=v_sc[4 * a :, s * HALF : (s + 1) * HALF],
+                        start=(a == 0),
+                        stop=(a == PASSES - 1),
+                    )
+
+        h_sum = []
+        for s in range(HALVES):
+            h_sum.append(held([P, PACK, HALF], F32, "h_sum%d" % s))
+            for t in range(PACK):
+                nc.scalar.activation(out=h_sum[s][:, t, :], in_=h_banks[PACK * s + t][:], func=COPY)
+
+        wb_grouped = held([P, N, PACK], BF16, "wb_grouped")
+        wb_q = held([P, N], U32, "wb_q")
+        wb_sc = held([P, N], U8, "wb_sc")
+        nc.vector.tensor_copy(out=wb_grouped[:], in_=wb_raw[:].rearrange("p j n -> p n j"))
+        for lo, hi in ((0, 512), (512, N)):
+            nc.vector.quantize_mx(
+                out=wb_q[:, lo:hi].bitcast(FP8X4),
+                scales=wb_sc[:, lo:hi],
+                in_=wb_grouped[:, lo:hi, :].rearrange("p n j -> p (n j)"),
+            )
+
+        h_q, h_sc = [], []
+        for s in range(HALVES):
+            h_grouped = held([P, HALF, PACK], BF16, "h_grouped%d" % s)
+            nc.vector.tensor_tensor(
+                out=h_grouped[:],
+                in0=h_sum[s][:].rearrange("p t s -> p s t"),
+                in1=gains[s][:].rearrange("p t s -> p s t"),
+                op=MULT,
+            )
+            h_q.append(held([P, HALF], U32, "h_q%d" % s))
+            h_sc.append(held([P, HALF], U8, "h_sc%d" % s))
+            nc.vector.quantize_mx(
+                out=h_q[s][:].bitcast(FP8X4), scales=h_sc[s][:], in_=h_grouped[:].rearrange("p s t -> p (s t)")
+            )
+
+        def dense(acc, s, n):
+            for a in range(PASSES):
+                cols = slice(s * HALF, (s + 1) * HALF)
+                nc.tensor.matmul_mx(
+                    out=acc[:],
+                    lhsT=wd[:, a, 2 * n * P : 2 * (n + 1) * P].bitcast(FP4X4),
+                    lhsT_scale=wd_sc[:, a, n * P : (n + 1) * P],
+                    rhs=v[a][s][:].bitcast(FP8X4),
+                    rhs_scale=v_sc[:, cols] if a == 0 else v_sc_low[:, a - 1, cols],
+                    start=(a == 0),
+                    stop=False,
+                )
+
+        def finish(acc, s, n):
+            nc.tensor.matmul_mx(
+                out=acc[:],
+                lhsT=wb_q[:, n * P : (n + 1) * P].bitcast(FP8X4),
+                lhsT_scale=wb_sc[:, n * P : (n + 1) * P],
+                rhs=h_q[s][:].bitcast(FP8X4),
+                rhs_scale=h_sc[s][:],
+                start=False,
+                stop=True,
+            )
+            result = stage.tile([P, HALF], F32, name="result")
+            nc.scalar.activation(out=result[:], in_=acc[:], func=IDENTITY, bias=bias[:, n : n + 1])
+            nc.sync.dma_start(out=out[n * P : (n + 1) * P, s * HALF : (s + 1) * HALF], in_=result[:])
+
+        tiles = [(s, n) for s in range(HALVES) for n in range(N_TILES)]
+        first = [bank(b) for b in range(BANKS)]
+        for b in range(BANKS):
+            dense(first[b], *tiles[b])
+        for b in range(BANKS):
+            finish(first[b], *tiles[b])
+        for b in range(len(tiles) - BANKS):
+            acc = bank(b)
+            dense(acc, *tiles[BANKS + b])
+            finish(acc, *tiles[BANKS + b])

@@ -16,6 +16,7 @@ FP4X4 = mybir.dt.float4_e2m1fn_x4
 COPY = mybir.ActivationFunctionType.Copy
 IDENTITY = mybir.ActivationFunctionType.Identity
 MULT = mybir.AluOpType.mult
+ADD = mybir.AluOpType.add
 
 P = 128
 PACK = 4
@@ -26,6 +27,7 @@ N_TILES = N // P
 QUADS = 4
 BANKS = 8
 SHIFT_ROWS = 112
+WB_SPLIT = 512
 
 
 def tile_list_tenant_adapter_queries_kernel(
@@ -34,7 +36,7 @@ def tile_list_tenant_adapter_queries_kernel(
     nc = tc.nc
     with ExitStack() as ctx:
         keep = ctx.enter_context(tc.tile_pool(name="keep", bufs=1))
-        stage = ctx.enter_context(tc.tile_pool(name="stage", bufs=12))
+        stage = ctx.enter_context(tc.tile_pool(name="stage", bufs=13))
         psum = ctx.enter_context(tc.psum_pool(name="psum", bufs=1))
 
         def held(shape, dtype, name):
@@ -45,6 +47,16 @@ def tile_list_tenant_adapter_queries_kernel(
 
         offsets = keep.tile([P, S // 16], U16, name="offsets")
         nc.sync.dma_start(offsets[:], offs)
+
+        wa_raw = [held([P, PACK, R], F32, "wa_raw%d" % a) for a in range(PASSES)]
+
+        def load_wa(a):
+            nc.sync.dma_start(
+                out=wa_raw[a][:],
+                in_=wa[a * P * PACK : (a + 1) * P * PACK, :].rearrange("(p j) c -> p j c", j=PACK),
+            )
+
+        load_wa(0)
 
         tab_sc = held([P, T], U8, "tab_sc")
         wd_sc = held([P, PASSES, N], U8, "wd_sc")
@@ -73,33 +85,31 @@ def tile_list_tenant_adapter_queries_kernel(
                     in_=v_sc[4 * a : 4 * a + SHIFT_ROWS, s * HALF : (s + 1) * HALF].bitcast(I32),
                 )
 
-        wa_raw, tab = [], []
+        tab = []
         for a in range(PASSES):
-            wa_raw.append(held([P, PACK, R], F32, "wa_raw%d" % a))
-            nc.sync.dma_start(
-                out=wa_raw[a][:],
-                in_=wa[a * P * PACK : (a + 1) * P * PACK, :].rearrange("(p j) c -> p j c", j=PACK),
-            )
+            if a > 0:
+                load_wa(a)
             tab.append(held([P, T], I32, "tab%d" % a))
             nc.sync.dma_start(out=tab[a][:], in_=tab_words[a].rearrange("p t i -> p (t i)").bitcast(I32))
         wd = held([P, PASSES, 2 * N], U8, "wd")
         nc.sync.dma_start(out=wd[:].bitcast(I32), in_=wd_words.rearrange("a p c -> p a c").bitcast(I32))
-        shift_scales(0)
-        wb_raw = held([P, PACK, N], F32, "wb_raw")
-        nc.sync.dma_start(out=wb_raw[:], in_=wb.rearrange("(p j) n -> p j n", j=PACK))
-        gains = []
-        bias = held([P, N_TILES], F32, "bias")
-        for s in range(HALVES):
-            gains.append(held([P, PACK, HALF], F32, "gain%d" % s))
+        gains = [held([P, PACK, HALF], F32, "gain%d" % s) for s in range(HALVES)]
+
+        def load_gain(s):
             nc.sync.dma_start(
                 out=gains[s][:],
                 in_=gain[:, s * HALF : (s + 1) * HALF].rearrange("(p j) s -> p j s", j=PACK),
             )
-            if s == 0:
-                shift_scales(1)
-                with nc.allow_non_contiguous_dma(reason="one bias value a partition"):
-                    nc.sync.dma_start(out=bias[:], in_=bq.rearrange("(c p) -> p c", p=P))
 
+        shift_scales(0)
+        load_gain(0)
+        wb_raw = held([P, PACK, N], F32, "wb_raw")
+        nc.sync.dma_start(out=wb_raw[:], in_=wb.rearrange("(p j) n -> p j n", j=PACK))
+        shift_scales(1)
+        bias = held([P, N_TILES], F32, "bias")
+        with nc.allow_non_contiguous_dma(reason="one bias value a partition"):
+            nc.sync.dma_start(out=bias[:], in_=bq.rearrange("(c p) -> p c", p=P))
+        load_gain(1)
 
         h_banks = [bank(b) for b in range(BANKS)]
         v = [[None] * HALVES for a in range(PASSES)]
@@ -117,22 +127,25 @@ def tile_list_tenant_adapter_queries_kernel(
             nc.vector.quantize_mx(
                 out=wa_q[:].bitcast(FP8X4), scales=wa_sc[:], in_=grouped[:].rearrange("p t m j -> p (t m j)")
             )
+            width = HALF // 2 if a == PASSES - 1 else HALF
             for s in range(HALVES):
                 v[a][s] = held([P, HALF], U32, "v%d_%d" % (a, s))
-                nc.vector.tensor_copy(
-                    out=v[a][s][:],
-                    in_=tab[a][:].bitcast(U32).indirect(offsets[:, s * HALF // 16 : (s + 1) * HALF // 16]),
-                )
-                for t in range(PACK):
-                    nc.tensor.matmul_mx(
-                        out=h_banks[PACK * s + t][:],
-                        lhsT=wa_q[:, t * P : (t + 1) * P].bitcast(FP8X4),
-                        lhsT_scale=wa_sc[:, t * P : (t + 1) * P],
-                        rhs=v[a][s][:].bitcast(FP8X4),
-                        rhs_scale=v_sc[4 * a :, s * HALF : (s + 1) * HALF],
-                        start=(a == 0),
-                        stop=(a == PASSES - 1),
+                for lo in range(0, HALF, width):
+                    first = s * HALF + lo
+                    nc.vector.tensor_copy(
+                        out=v[a][s][:, lo : lo + width],
+                        in_=tab[a][:].bitcast(U32).indirect(offsets[:, first // 16 : (first + width) // 16]),
                     )
+                    for t in range(PACK):
+                        nc.tensor.matmul_mx(
+                            out=h_banks[PACK * s + t][:, lo : lo + width],
+                            lhsT=wa_q[:, t * P : (t + 1) * P].bitcast(FP8X4),
+                            lhsT_scale=wa_sc[:, t * P : (t + 1) * P],
+                            rhs=v[a][s][:, lo : lo + width].bitcast(FP8X4),
+                            rhs_scale=v_sc[4 * a :, first : first + width],
+                            start=(a == 0),
+                            stop=(a == PASSES - 1 and lo + width == HALF),
+                        )
 
         h_sum = []
         for s in range(HALVES):
@@ -140,24 +153,17 @@ def tile_list_tenant_adapter_queries_kernel(
             for t in range(PACK):
                 nc.scalar.activation(out=h_sum[s][:, t, :], in_=h_banks[PACK * s + t][:], func=COPY)
 
-        wb_grouped = held([P, N, PACK], BF16, "wb_grouped")
-        wb_q = held([P, N], U32, "wb_q")
-        wb_sc = held([P, N], U8, "wb_sc")
-        nc.vector.tensor_copy(out=wb_grouped[:], in_=wb_raw[:].rearrange("p j n -> p n j"))
-        for lo, hi in ((0, 512), (512, N)):
-            nc.vector.quantize_mx(
-                out=wb_q[:, lo:hi].bitcast(FP8X4),
-                scales=wb_sc[:, lo:hi],
-                in_=wb_grouped[:, lo:hi, :].rearrange("p n j -> p (n j)"),
-            )
+        def by_fours(ap, form):
+            return ap.rearrange(form + " -> p c t i", i=PACK)
 
         h_q, h_sc = [], []
-        for s in range(HALVES):
+
+        def quantize_h(s):
             h_grouped = held([P, HALF, PACK], BF16, "h_grouped%d" % s)
             nc.vector.tensor_tensor(
-                out=h_grouped[:],
-                in0=h_sum[s][:].rearrange("p t s -> p s t"),
-                in1=gains[s][:].rearrange("p t s -> p s t"),
+                out=by_fours(h_grouped[:], "p (c i) t"),
+                in0=by_fours(h_sum[s][:], "p t (c i)"),
+                in1=by_fours(gains[s][:], "p t (c i)"),
                 op=MULT,
             )
             h_q.append(held([P, HALF], U32, "h_q%d" % s))
@@ -165,6 +171,24 @@ def tile_list_tenant_adapter_queries_kernel(
             nc.vector.quantize_mx(
                 out=h_q[s][:].bitcast(FP8X4), scales=h_sc[s][:], in_=h_grouped[:].rearrange("p s t -> p (s t)")
             )
+
+        quantize_h(0)
+        wb_q = held([P, N], U32, "wb_q")
+        wb_sc = held([P, N], U8, "wb_sc")
+        for lo, hi in ((0, WB_SPLIT), (WB_SPLIT, N)):
+            wb_grouped = held([P, hi - lo, PACK], BF16, "wb_grouped%d" % lo)
+            dst = by_fours(wb_grouped[:], "p (c i) t")
+            src = by_fours(wb_raw[:, :, lo:hi], "p t (c i)")
+            if lo == 0:
+                nc.vector.tensor_copy(out=dst, in_=src)
+            else:
+                nc.scalar.activation(out=dst, in_=src, func=COPY)
+            nc.vector.quantize_mx(
+                out=wb_q[:, lo:hi].bitcast(FP8X4),
+                scales=wb_sc[:, lo:hi],
+                in_=wb_grouped[:].rearrange("p n j -> p (n j)"),
+            )
+        quantize_h(1)
 
         def dense(acc, s, n):
             for a in range(PASSES):
@@ -189,17 +213,32 @@ def tile_list_tenant_adapter_queries_kernel(
                 start=False,
                 stop=True,
             )
-            result = stage.tile([P, HALF], F32, name="result")
-            nc.scalar.activation(out=result[:], in_=acc[:], func=IDENTITY, bias=bias[:, n : n + 1])
-            nc.sync.dma_start(out=out[n * P : (n + 1) * P, s * HALF : (s + 1) * HALF], in_=result[:])
+            pieces = 2 if (s, n) == (HALVES - 1, N_TILES - 1) else 1
+            width = HALF // pieces
+            for i in range(pieces):
+                result = stage.tile([P, width], F32, name="result")
+                sums = acc[:, i * width : (i + 1) * width]
+                if s == 1 and n in (1, 4):
+                    nc.vector.tensor_scalar(
+                        out=result[:], in0=sums, scalar1=bias[:, n : n + 1], scalar2=None, op0=ADD
+                    )
+                else:
+                    nc.scalar.activation(out=result[:], in_=sums, func=IDENTITY, bias=bias[:, n : n + 1])
+                col = s * HALF + i * width
+                nc.sync.dma_start(out=out[n * P : (n + 1) * P, col : col + width], in_=result[:])
 
         tiles = [(s, n) for s in range(HALVES) for n in range(N_TILES)]
-        first = [bank(b) for b in range(BANKS)]
-        for b in range(BANKS):
-            dense(first[b], *tiles[b])
-        for b in range(BANKS):
-            finish(first[b], *tiles[b])
-        for b in range(len(tiles) - BANKS):
-            acc = bank(b)
-            dense(acc, *tiles[BANKS + b])
-            finish(acc, *tiles[BANKS + b])
+        accs = [bank(b) for b in range(BANKS)]
+        for i in range(BANKS):
+            dense(accs[i], *tiles[i])
+        for i in range(N_TILES):
+            finish(accs[i], *tiles[i])
+        for i in range(BANKS, BANKS + 1):
+            accs.append(bank(i - BANKS))
+            dense(accs[i], *tiles[i])
+        for i in range(N_TILES, BANKS + 1):
+            finish(accs[i], *tiles[i])
+        for i in range(BANKS + 1, len(tiles)):
+            accs.append(bank(i - BANKS))
+            dense(accs[i], *tiles[i])
+            finish(accs[i], *tiles[i])

@@ -28,6 +28,7 @@ QUADS = 4
 BANKS = 8
 SHIFT_ROWS = 112
 WB_SPLIT = 512
+WD_SPLIT = 384
 
 
 def tile_list_tenant_adapter_queries_kernel(
@@ -69,6 +70,7 @@ def tile_list_tenant_adapter_queries_kernel(
                 out=tab_sc[32 * q : 32 * q + 16, :].bitcast(I32),
                 in_=tab_scales[:, 4 * q : 4 * q + 4, :].bitcast(I32),
             )
+
         for q in range(QUADS):
             nc.gpsimd.dma_start(
                 out=wd_sc[32 * q : 32 * q + 4, :, :].bitcast(I32),
@@ -78,12 +80,6 @@ def tile_list_tenant_adapter_queries_kernel(
         v_sc = held([P, S], U8, "v_sc")
         nc.vector.tensor_copy(out=v_sc[:], in_=tab_sc[:].indirect(offsets[:]))
 
-        def shift_scales(s):
-            for a in range(1, PASSES):
-                nc.sync.dma_start(
-                    out=v_sc_low[0:SHIFT_ROWS, a - 1, s * HALF : (s + 1) * HALF].bitcast(I32),
-                    in_=v_sc[4 * a : 4 * a + SHIFT_ROWS, s * HALF : (s + 1) * HALF].bitcast(I32),
-                )
 
         tab = []
         for a in range(PASSES):
@@ -92,7 +88,14 @@ def tile_list_tenant_adapter_queries_kernel(
             tab.append(held([P, T], I32, "tab%d" % a))
             nc.sync.dma_start(out=tab[a][:], in_=tab_words[a].rearrange("p t i -> p (t i)").bitcast(I32))
         wd = held([P, PASSES, 2 * N], U8, "wd")
-        nc.sync.dma_start(out=wd[:].bitcast(I32), in_=wd_words.rearrange("a p c -> p a c").bitcast(I32))
+
+        def load_wd(lo, hi):
+            nc.sync.dma_start(
+                out=wd[:, :, 2 * lo : 2 * hi].bitcast(I32),
+                in_=wd_words[:, :, 2 * lo : 2 * hi].rearrange("a p c -> p a c").bitcast(I32),
+            )
+
+        load_wd(0, WD_SPLIT)
         gains = [held([P, PACK, HALF], F32, "gain%d" % s) for s in range(HALVES)]
 
         def load_gain(s):
@@ -101,11 +104,15 @@ def tile_list_tenant_adapter_queries_kernel(
                 in_=gain[:, s * HALF : (s + 1) * HALF].rearrange("(p j) s -> p j s", j=PACK),
             )
 
-        shift_scales(0)
+        for a in range(1, PASSES):
+            nc.sync.dma_start(
+                out=v_sc_low[0:SHIFT_ROWS, a - 1, :].bitcast(I32),
+                in_=v_sc[4 * a : 4 * a + SHIFT_ROWS, :].bitcast(I32),
+            )
+        load_wd(WD_SPLIT, N)
         load_gain(0)
         wb_raw = held([P, PACK, N], F32, "wb_raw")
         nc.sync.dma_start(out=wb_raw[:], in_=wb.rearrange("(p j) n -> p j n", j=PACK))
-        shift_scales(1)
         bias = held([P, N_TILES], F32, "bias")
         with nc.allow_non_contiguous_dma(reason="one bias value a partition"):
             nc.sync.dma_start(out=bias[:], in_=bq.rearrange("(c p) -> p c", p=P))
@@ -117,11 +124,11 @@ def tile_list_tenant_adapter_queries_kernel(
             grouped = held([P, PACK, P, PACK], BF16, "wa_grouped%d" % a)
             dst = grouped[:].rearrange("p t m j -> p m j t")
             src = wa_raw[a][:].rearrange("p j (m t) -> p m j t", t=PACK)
+            nc.scalar.activation(out=dst[:, :, :, :2], in_=src[:, :, :, :2], func=COPY)
             if a < PASSES - 1:
-                nc.scalar.activation(out=dst, in_=src, func=COPY)
+                nc.scalar.activation(out=dst[:, :, :, 2:], in_=src[:, :, :, 2:], func=COPY)
             else:
-                nc.scalar.activation(out=dst[:, : P // 2], in_=src[:, : P // 2], func=COPY)
-                nc.vector.tensor_copy(out=dst[:, P // 2 :], in_=src[:, P // 2 :])
+                nc.vector.tensor_copy(out=dst[:, :, :, 2:], in_=src[:, :, :, 2:])
             wa_q = held([P, R], U32, "wa_q%d" % a)
             wa_sc = held([P, R], U8, "wa_sc%d" % a)
             nc.vector.quantize_mx(
@@ -213,7 +220,7 @@ def tile_list_tenant_adapter_queries_kernel(
                 start=False,
                 stop=True,
             )
-            pieces = 2 if (s, n) == (HALVES - 1, N_TILES - 1) else 1
+            pieces = 1
             width = HALF // pieces
             for i in range(pieces):
                 result = stage.tile([P, width], F32, name="result")
@@ -238,7 +245,7 @@ def tile_list_tenant_adapter_queries_kernel(
             dense(accs[i], *tiles[i])
         for i in range(N_TILES, BANKS + 1):
             finish(accs[i], *tiles[i])
-        for i in range(BANKS + 1, len(tiles)):
-            accs.append(bank(i - BANKS))
+        for i, b in ((9, 1), (10, 6), (11, 7)):
+            accs.append(bank(b))
             dense(accs[i], *tiles[i])
             finish(accs[i], *tiles[i])

@@ -62,11 +62,11 @@ def tile_list_tenant_adapter_queries_kernel(
         tab_sc = held([P, T], U8, "tab_sc")
         wd_sc = held([P, PASSES, N], U8, "wd_sc")
         v_sc_low = held([P, PASSES - 1, S], U8, "v_sc_low")
-        nc.gpsimd.memset(tab_sc[:].bitcast(I32), 0)
+        nc.vector.memset(tab_sc[:].bitcast(I32), 0)
         nc.vector.memset(wd_sc[:].bitcast(I32), 0)
         nc.vector.memset(v_sc_low[:].bitcast(I32), 0)
         for q in range(QUADS):
-            nc.sync.dma_start(
+            nc.gpsimd.dma_start(
                 out=tab_sc[32 * q : 32 * q + 16, :].bitcast(I32),
                 in_=tab_scales[:, 4 * q : 4 * q + 4, :].bitcast(I32),
             )

@@ -59,6 +59,15 @@ def tile_list_tenant_adapter_queries_kernel(
 
         load_wa(0)
 
+        bias_rows = held([P, 256], F32, "bias_rows")
+        bias = held([P, 256], F32, "bias")
+        nc.vector.memset(bias_rows[:], 0.0)
+        nc.scalar.dma_start(
+            out=bias_rows[0:P:32, 0 : 32 * N_TILES].rearrange("q (c i) -> q c i", i=32),
+            in_=bq.rearrange("(c q i) -> q c i", q=QUADS, i=32),
+        )
+        nc.vector.transpose(bias[:], bias_rows[:])
+
         tab_sc = held([P, T], U8, "tab_sc")
         wd_sc = held([P, PASSES, N], U8, "wd_sc")
         v_sc_low = held([P, PASSES - 1, S], U8, "v_sc_low")
@@ -113,9 +122,6 @@ def tile_list_tenant_adapter_queries_kernel(
         load_gain(0)
         wb_raw = held([P, PACK, N], F32, "wb_raw")
         nc.sync.dma_start(out=wb_raw[:], in_=wb.rearrange("(p j) n -> p j n", j=PACK))
-        bias = held([P, N_TILES], F32, "bias")
-        with nc.allow_non_contiguous_dma(reason="one bias value a partition"):
-            nc.sync.dma_start(out=bias[:], in_=bq.rearrange("(c p) -> p c", p=P))
         load_gain(1)
 
         h_banks = [bank(b) for b in range(BANKS)]
@@ -227,10 +233,10 @@ def tile_list_tenant_adapter_queries_kernel(
                 sums = acc[:, i * width : (i + 1) * width]
                 if s == 1 and n in (1, 4):
                     nc.vector.tensor_scalar(
-                        out=result[:], in0=sums, scalar1=bias[:, n : n + 1], scalar2=None, op0=ADD
+                        out=result[:], in0=sums, scalar1=bias[:, 32 * n : 32 * n + 1], scalar2=None, op0=ADD
                     )
                 else:
-                    nc.scalar.activation(out=result[:], in_=sums, func=IDENTITY, bias=bias[:, n : n + 1])
+                    nc.scalar.activation(out=result[:], in_=sums, func=IDENTITY, bias=bias[:, 32 * n : 32 * n + 1])
                 col = s * HALF + i * width
                 nc.sync.dma_start(out=out[n * P : (n + 1) * P, col : col + width], in_=result[:])
 

@@ -27,8 +27,7 @@ N_TILES = N // P
 QUADS = 4
 BANKS = 8
 SHIFT_ROWS = 112
-WB_SPLIT = 512
-WD_SPLIT = 384
+WB_PART = 256
 
 
 def tile_list_tenant_adapter_queries_kernel(
@@ -104,7 +103,7 @@ def tile_list_tenant_adapter_queries_kernel(
                 in_=wd_words[:, :, 2 * lo : 2 * hi].rearrange("a p c -> p a c").bitcast(I32),
             )
 
-        load_wd(0, WD_SPLIT)
+        load_wd(0, N)
         gains = [held([P, PACK, HALF], F32, "gain%d" % s) for s in range(HALVES)]
 
         def load_gain(s):
@@ -118,7 +117,6 @@ def tile_list_tenant_adapter_queries_kernel(
                 out=v_sc_low[0:SHIFT_ROWS, a - 1, :].bitcast(I32),
                 in_=v_sc[4 * a : 4 * a + SHIFT_ROWS, :].bitcast(I32),
             )
-        load_wd(WD_SPLIT, N)
         load_gain(0)
         wb_raw = held([P, PACK, N], F32, "wb_raw")
         nc.sync.dma_start(out=wb_raw[:], in_=wb.rearrange("(p j) n -> p j n", j=PACK))
@@ -188,11 +186,12 @@ def tile_list_tenant_adapter_queries_kernel(
         quantize_h(0)
         wb_q = held([P, N], U32, "wb_q")
         wb_sc = held([P, N], U8, "wb_sc")
-        for lo, hi in ((0, WB_SPLIT), (WB_SPLIT, N)):
+        for lo in (0, 2 * WB_PART, WB_PART):
+            hi = lo + WB_PART
             wb_grouped = held([P, hi - lo, PACK], BF16, "wb_grouped%d" % lo)
             dst = by_fours(wb_grouped[:], "p (c i) t")
             src = by_fours(wb_raw[:, :, lo:hi], "p t (c i)")
-            if lo == 0:
+            if hi < N:
                 nc.vector.tensor_copy(out=dst, in_=src)
             else:
                 nc.scalar.activation(out=dst, in_=src, func=COPY)
@@ -226,12 +225,12 @@ def tile_list_tenant_adapter_queries_kernel(
                 start=False,
                 stop=True,
             )
-            pieces = 1
+            pieces = 2 if (s, n) == (HALVES - 1, N_TILES - 1) else 1
             width = HALF // pieces
             for i in range(pieces):
                 result = stage.tile([P, width], F32, name="result")
                 sums = acc[:, i * width : (i + 1) * width]
-                if s == 1 and n in (1, 4):
+                if s == 1 and n in (1, 3):
                     nc.vector.tensor_scalar(
                         out=result[:], in0=sums, scalar1=bias[:, 32 * n : 32 * n + 1], scalar2=None, op0=ADD
                     )
@@ -242,16 +241,19 @@ def tile_list_tenant_adapter_queries_kernel(
 
         tiles = [(s, n) for s in range(HALVES) for n in range(N_TILES)]
         accs = [bank(b) for b in range(BANKS)]
-        for i in range(BANKS):
+        for i in range(BANKS - 1):
             dense(accs[i], *tiles[i])
-        for i in range(N_TILES):
+        finish(accs[0], *tiles[0])
+        finish(accs[1], *tiles[1])
+        dense(accs[BANKS - 1], *tiles[BANKS - 1])
+        for i in range(2, N_TILES):
             finish(accs[i], *tiles[i])
-        for i in range(BANKS, BANKS + 1):
+        for i in (8, 9):
             accs.append(bank(i - BANKS))
             dense(accs[i], *tiles[i])
-        for i in range(N_TILES, BANKS + 1):
+        for i in range(N_TILES, 10):
             finish(accs[i], *tiles[i])
-        for i, b in ((9, 1), (10, 6), (11, 7)):
+        for i, b in ((10, 2), (11, 6)):
             accs.append(bank(b))
             dense(accs[i], *tiles[i])
             finish(accs[i], *tiles[i])

@@ -48,6 +48,23 @@ def tile_list_tenant_adapter_queries_kernel(
         offsets = keep.tile([P, S // 16], U16, name="offsets")
         nc.sync.dma_start(offsets[:], offs)
 
+        tab_sc = held([P, T], U8, "tab_sc")
+        wd_sc = held([P, PASSES, N], U8, "wd_sc")
+        v_sc_low = held([P, PASSES - 1, S], U8, "v_sc_low")
+
+        def clear(words):
+            last = words.shape[1] - 1
+            nc.vector.memset(words[:, :last], 0)
+            nc.vector.memset(words[:, last:], 0)
+
+        nc.vector.memset(tab_sc[:].bitcast(I32), 0)
+        for q in range(QUADS):
+            nc.gpsimd.dma_start(
+                out=tab_sc[32 * q : 32 * q + 16, :].bitcast(I32),
+                in_=tab_scales[:, 4 * q : 4 * q + 4, :].bitcast(I32),
+            )
+        clear(wd_sc[:].rearrange("p a n -> p (a n)").bitcast(I32))
+
         wa_raw = [held([P, PACK, R], F32, "wa_raw%d" % a) for a in range(PASSES)]
 
         def load_wa(a):
@@ -56,45 +73,50 @@ def tile_list_tenant_adapter_queries_kernel(
                 in_=wa[a * P * PACK : (a + 1) * P * PACK, :].rearrange("(p j) c -> p j c", j=PACK),
             )
 
+        tab = [held([P, T], I32, "tab%d" % a) for a in range(PASSES)]
+
+        def load_tab(a):
+            nc.sync.dma_start(out=tab[a][:], in_=tab_words[a].rearrange("p t i -> p (t i)").bitcast(I32))
+
+        load_tab(0)
         load_wa(0)
+        for a in range(1, PASSES):
+            load_wa(a)
+            if a == 1:
+                for q in range(QUADS):
+                    nc.sync.dma_start(
+                        out=wd_sc[32 * q : 32 * q + 4, :, :].bitcast(I32),
+                        in_=wd_scales[:, 4 * q : 4 * q + 4, :].rearrange("a r n -> r a n").bitcast(I32),
+                    )
+            load_tab(a)
 
         bias_rows = held([P, 256], F32, "bias_rows")
         bias = held([P, 256], F32, "bias")
-        nc.vector.memset(bias_rows[:], 0.0)
+        clear(bias_rows[:].bitcast(I32))
         nc.scalar.dma_start(
             out=bias_rows[0:P:32, 0 : 32 * N_TILES].rearrange("q (c i) -> q c i", i=32),
             in_=bq.rearrange("(c q i) -> q c i", q=QUADS, i=32),
         )
         nc.vector.transpose(bias[:], bias_rows[:])
 
-        tab_sc = held([P, T], U8, "tab_sc")
-        wd_sc = held([P, PASSES, N], U8, "wd_sc")
-        v_sc_low = held([P, PASSES - 1, S], U8, "v_sc_low")
-        nc.vector.memset(tab_sc[:].bitcast(I32), 0)
-        nc.vector.memset(wd_sc[:].bitcast(I32), 0)
-        nc.vector.memset(v_sc_low[:].bitcast(I32), 0)
-        for q in range(QUADS):
-            nc.gpsimd.dma_start(
-                out=tab_sc[32 * q : 32 * q + 16, :].bitcast(I32),
-                in_=tab_scales[:, 4 * q : 4 * q + 4, :].bitcast(I32),
+        clear(v_sc_low[:].rearrange("p a s -> p (a s)").bitcast(I32))
+
+        v = [[held([P, HALF], U32, "v%d_%d" % (a, s)) for s in range(HALVES)] for a in range(PASSES)]
+
+        def gather(a, s, lo, width):
+            first = s * HALF + lo
+            nc.vector.tensor_copy(
+                out=v[a][s][:, lo : lo + width],
+                in_=tab[a][:].bitcast(U32).indirect(offsets[:, first // 16 : (first + width) // 16]),
             )
 
-        for q in range(QUADS):
-            nc.gpsimd.dma_start(
-                out=wd_sc[32 * q : 32 * q + 4, :, :].bitcast(I32),
-                in_=wd_scales[:, 4 * q : 4 * q + 4, :].rearrange("a r n -> r a n").bitcast(I32),
-            )
+        for s in range(HALVES):
+            gather(0, s, 0, HALF)
 
         v_sc = held([P, S], U8, "v_sc")
         nc.vector.tensor_copy(out=v_sc[:], in_=tab_sc[:].indirect(offsets[:]))
 
 
-        tab = []
-        for a in range(PASSES):
-            if a > 0:
-                load_wa(a)
-            tab.append(held([P, T], I32, "tab%d" % a))
-            nc.sync.dma_start(out=tab[a][:], in_=tab_words[a].rearrange("p t i -> p (t i)").bitcast(I32))
         wd = held([P, PASSES, 2 * N], U8, "wd")
 
         def load_wd(lo, hi):
@@ -123,7 +145,6 @@ def tile_list_tenant_adapter_queries_kernel(
         load_gain(1)
 
         h_banks = [bank(b) for b in range(BANKS)]
-        v = [[None] * HALVES for a in range(PASSES)]
         for a in range(PASSES):
             grouped = held([P, PACK, P, PACK], BF16, "wa_grouped%d" % a)
             dst = grouped[:].rearrange("p t m j -> p m j t")
@@ -140,13 +161,10 @@ def tile_list_tenant_adapter_queries_kernel(
             )
             width = HALF // 2 if a == PASSES - 1 else HALF
             for s in range(HALVES):
-                v[a][s] = held([P, HALF], U32, "v%d_%d" % (a, s))
                 for lo in range(0, HALF, width):
                     first = s * HALF + lo
-                    nc.vector.tensor_copy(
-                        out=v[a][s][:, lo : lo + width],
-                        in_=tab[a][:].bitcast(U32).indirect(offsets[:, first // 16 : (first + width) // 16]),
-                    )
+                    if a > 0:
+                        gather(a, s, lo, width)
                     for t in range(PACK):
                         nc.tensor.matmul_mx(
                             out=h_banks[PACK * s + t][:, lo : lo + width],

@@ -46,7 +46,6 @@ def tile_list_tenant_adapter_queries_kernel(
             return psum.tile([P, HALF], F32, name="bank%d" % b)
 
         offsets = keep.tile([P, S // 16], U16, name="offsets")
-        nc.sync.dma_start(offsets[:], offs)
 
         tab_sc = held([P, T], U8, "tab_sc")
         wd_sc = held([P, PASSES, N], U8, "wd_sc")
@@ -79,14 +78,15 @@ def tile_list_tenant_adapter_queries_kernel(
             nc.sync.dma_start(out=tab[a][:], in_=tab_words[a].rearrange("p t i -> p (t i)").bitcast(I32))
 
         load_tab(0)
+        nc.sync.dma_start(offsets[:], offs)
         load_wa(0)
         for a in range(1, PASSES):
             load_wa(a)
             if a == 1:
-                for q in range(QUADS):
+                for r in range(4):
                     nc.sync.dma_start(
-                        out=wd_sc[32 * q : 32 * q + 4, :, :].bitcast(I32),
-                        in_=wd_scales[:, 4 * q : 4 * q + 4, :].rearrange("a r n -> r a n").bitcast(I32),
+                        out=wd_sc[r:P:32, :, :].bitcast(I32),
+                        in_=wd_scales[:, r:16:4, :].rearrange("a q n -> q a n").bitcast(I32),
                     )
             load_tab(a)
 
@@ -156,9 +156,13 @@ def tile_list_tenant_adapter_queries_kernel(
                 nc.vector.tensor_copy(out=dst[:, :, :, 2:], in_=src[:, :, :, 2:])
             wa_q = held([P, R], U32, "wa_q%d" % a)
             wa_sc = held([P, R], U8, "wa_sc%d" % a)
-            nc.vector.quantize_mx(
-                out=wa_q[:].bitcast(FP8X4), scales=wa_sc[:], in_=grouped[:].rearrange("p t m j -> p (t m j)")
-            )
+            slot_runs = ((0, PACK),) if a < PASSES - 1 else ((2, PACK), (0, 2))
+            for t0, t1 in slot_runs:
+                nc.vector.quantize_mx(
+                    out=wa_q[:, t0 * P : t1 * P].bitcast(FP8X4),
+                    scales=wa_sc[:, t0 * P : t1 * P],
+                    in_=grouped[:, t0:t1].rearrange("p t m j -> p (t m j)"),
+                )
             width = HALF // 2 if a == PASSES - 1 else HALF
             for s in range(HALVES):
                 for lo in range(0, HALF, width):

@@ -28,6 +28,7 @@ QUADS = 4
 BANKS = 8
 SHIFT_ROWS = 112
 WB_PART = 256
+EARLY_N = 256
 
 
 def tile_list_tenant_adapter_queries_kernel(
@@ -47,24 +48,29 @@ def tile_list_tenant_adapter_queries_kernel(
 
         offsets = keep.tile([P, S // 16], U16, name="offsets")
 
+        col_parts = ((0, EARLY_N), (EARLY_N, N))
         tab_sc = held([P, T], U8, "tab_sc")
-        wd_sc = held([P, PASSES, N], U8, "wd_sc")
+        wd_sc = [held([P, PASSES, hi - lo], U8, "wd_sc%d" % lo) for lo, hi in col_parts]
+        wd = [held([P, PASSES, 2 * (hi - lo)], U8, "wd%d" % lo) for lo, hi in col_parts]
+        v_sc = held([P, S], U8, "v_sc")
         v_sc_low = held([P, PASSES - 1, S], U8, "v_sc_low")
+        wa_raw = [held([P, PACK, R], F32, "wa_raw%d" % a) for a in range(PASSES)]
+        tab = [held([P, T], I32, "tab%d" % a) for a in range(PASSES)]
+        gains = [held([P, PACK, HALF], F32, "gain%d" % s) for s in range(HALVES)]
+        wb_raw = [held([P, PACK, hi - lo], F32, "wb_raw%d" % lo) for lo, hi in col_parts]
+        v = [[held([P, HALF], U32, "v%d_%d" % (a, s)) for s in range(HALVES)] for a in range(PASSES)]
 
         def clear(words):
             last = words.shape[1] - 1
             nc.vector.memset(words[:, :last], 0)
             nc.vector.memset(words[:, last:], 0)
 
-        nc.vector.memset(tab_sc[:].bitcast(I32), 0)
-        for q in range(QUADS):
-            nc.gpsimd.dma_start(
-                out=tab_sc[32 * q : 32 * q + 16, :].bitcast(I32),
-                in_=tab_scales[:, 4 * q : 4 * q + 4, :].bitcast(I32),
-            )
-        clear(wd_sc[:].rearrange("p a n -> p (a n)").bitcast(I32))
-
-        wa_raw = [held([P, PACK, R], F32, "wa_raw%d" % a) for a in range(PASSES)]
+        def load_tab_scales():
+            for q in range(QUADS):
+                nc.gpsimd.dma_start(
+                    out=tab_sc[32 * q : 32 * q + 16, :].bitcast(I32),
+                    in_=tab_scales[:, 4 * q : 4 * q + 4, :].bitcast(I32),
+                )
 
         def load_wa(a):
             nc.sync.dma_start(
@@ -72,61 +78,27 @@ def tile_list_tenant_adapter_queries_kernel(
                 in_=wa[a * P * PACK : (a + 1) * P * PACK, :].rearrange("(p j) c -> p j c", j=PACK),
             )
 
-        tab = [held([P, T], I32, "tab%d" % a) for a in range(PASSES)]
-
         def load_tab(a):
             nc.sync.dma_start(out=tab[a][:], in_=tab_words[a].rearrange("p t i -> p (t i)").bitcast(I32))
 
-        load_tab(0)
-        nc.sync.dma_start(offsets[:], offs)
-        load_wa(0)
-        for a in range(1, PASSES):
-            load_wa(a)
-            if a == 1:
-                for r in range(4):
-                    nc.sync.dma_start(
-                        out=wd_sc[r:P:32, :, :].bitcast(I32),
-                        in_=wd_scales[:, r:16:4, :].rearrange("a q n -> q a n").bitcast(I32),
-                    )
-            load_tab(a)
+        def load_wd_scales(part):
+            lo, hi = col_parts[part]
+            for r in range(4):
+                nc.sync.dma_start(
+                    out=wd_sc[part][r:P:32, :, :].bitcast(I32),
+                    in_=wd_scales[:, r:16:4, lo:hi].rearrange("a q n -> q a n").bitcast(I32),
+                )
 
-        bias_rows = held([P, 256], F32, "bias_rows")
-        bias = held([P, 256], F32, "bias")
-        clear(bias_rows[:].bitcast(I32))
-        nc.scalar.dma_start(
-            out=bias_rows[0:P:32, 0 : 32 * N_TILES].rearrange("q (c i) -> q c i", i=32),
-            in_=bq.rearrange("(c q i) -> q c i", q=QUADS, i=32),
-        )
-        nc.vector.transpose(bias[:], bias_rows[:])
-
-        clear(v_sc_low[:].rearrange("p a s -> p (a s)").bitcast(I32))
-
-        v = [[held([P, HALF], U32, "v%d_%d" % (a, s)) for s in range(HALVES)] for a in range(PASSES)]
-
-        def gather(a, s, lo, width):
-            first = s * HALF + lo
-            nc.vector.tensor_copy(
-                out=v[a][s][:, lo : lo + width],
-                in_=tab[a][:].bitcast(U32).indirect(offsets[:, first // 16 : (first + width) // 16]),
-            )
-
-        for s in range(HALVES):
-            gather(0, s, 0, HALF)
-
-        v_sc = held([P, S], U8, "v_sc")
-        nc.vector.tensor_copy(out=v_sc[:], in_=tab_sc[:].indirect(offsets[:]))
-
-
-        wd = held([P, PASSES, 2 * N], U8, "wd")
-
-        def load_wd(lo, hi):
+        def load_wd(part):
+            lo, hi = col_parts[part]
             nc.sync.dma_start(
-                out=wd[:, :, 2 * lo : 2 * hi].bitcast(I32),
+                out=wd[part][:].bitcast(I32),
                 in_=wd_words[:, :, 2 * lo : 2 * hi].rearrange("a p c -> p a c").bitcast(I32),
             )
 
-        load_wd(0, N)
-        gains = [held([P, PACK, HALF], F32, "gain%d" % s) for s in range(HALVES)]
+        def load_wb(part):
+            lo, hi = col_parts[part]
+            nc.sync.dma_start(out=wb_raw[part][:], in_=wb[:, lo:hi].rearrange("(p j) n -> p j n", j=PACK))
 
         def load_gain(s):
             nc.sync.dma_start(
@@ -134,110 +106,201 @@ def tile_list_tenant_adapter_queries_kernel(
                 in_=gain[:, s * HALF : (s + 1) * HALF].rearrange("(p j) s -> p j s", j=PACK),
             )
 
+        def gather(a, s):
+            nc.vector.tensor_copy(
+                out=v[a][s][:],
+                in_=tab[a][:].bitcast(U32).indirect(offsets[:, s * HALF // 16 : (s + 1) * HALF // 16]),
+            )
+
+        nc.vector.memset(tab_sc[:].bitcast(I32), 0)
+        load_tab(0)
+        nc.sync.dma_start(offsets[:], offs)
+        load_tab_scales()
+        clear(wd_sc[0][:].rearrange("p a n -> p (a n)").bitcast(I32))
+        load_wa(0)
+        load_wa(1)
+        load_wd_scales(0)
+        load_tab(1)
+        load_wd(0)
+        load_tab(2)
+
+        clear(v_sc_low[:].rearrange("p a s -> p (a s)").bitcast(I32))
+        clear(wd_sc[1][:].rearrange("p a n -> p (a n)").bitcast(I32))
+
+        for s in range(HALVES):
+            gather(0, s)
+        nc.vector.tensor_copy(out=v_sc[:], in_=tab_sc[:].indirect(offsets[:]))
+
         for a in range(1, PASSES):
             nc.sync.dma_start(
                 out=v_sc_low[0:SHIFT_ROWS, a - 1, :].bitcast(I32),
                 in_=v_sc[4 * a : 4 * a + SHIFT_ROWS, :].bitcast(I32),
             )
+        load_wa(2)
+        load_tab(3)
+        load_wa(3)
+        load_wd(1)
+        load_wd_scales(1)
+        bias_rows = held([P, 256], F32, "bias_rows")
+        bias = held([P, 256], F32, "bias")
+        clear(bias_rows[:].bitcast(I32))
+        nc.sync.dma_start(
+            out=bias_rows[0:P:32, 0 : 32 * N_TILES].rearrange("q (c i) -> q c i", i=32),
+            in_=bq.rearrange("(c q i) -> q c i", q=QUADS, i=32),
+        )
+        load_wb(0)
         load_gain(0)
-        wb_raw = held([P, PACK, N], F32, "wb_raw")
-        nc.sync.dma_start(out=wb_raw[:], in_=wb.rearrange("(p j) n -> p j n", j=PACK))
+        load_wb(1)
         load_gain(1)
 
-        h_banks = [bank(b) for b in range(BANKS)]
-        for a in range(PASSES):
+        wa_q = [held([P, R], U32, "wa_q%d" % a) for a in range(PASSES)]
+        wa_sc = [held([P, R], U8, "wa_sc%d" % a) for a in range(PASSES)]
+
+        def quantize_wa(a, shared):
             grouped = held([P, PACK, P, PACK], BF16, "wa_grouped%d" % a)
             dst = grouped[:].rearrange("p t m j -> p m j t")
             src = wa_raw[a][:].rearrange("p j (m t) -> p m j t", t=PACK)
             nc.scalar.activation(out=dst[:, :, :, :2], in_=src[:, :, :, :2], func=COPY)
-            if a < PASSES - 1:
-                nc.scalar.activation(out=dst[:, :, :, 2:], in_=src[:, :, :, 2:], func=COPY)
-            else:
+            if shared:
                 nc.vector.tensor_copy(out=dst[:, :, :, 2:], in_=src[:, :, :, 2:])
-            wa_q = held([P, R], U32, "wa_q%d" % a)
-            wa_sc = held([P, R], U8, "wa_sc%d" % a)
-            slot_runs = ((0, PACK),) if a < PASSES - 1 else ((2, PACK), (0, 2))
-            for t0, t1 in slot_runs:
+            else:
+                nc.scalar.activation(out=dst[:, :, :, 2:], in_=src[:, :, :, 2:], func=COPY)
+            for t0, t1 in ((2, PACK), (0, 2)) if shared else ((0, PACK),):
                 nc.vector.quantize_mx(
-                    out=wa_q[:, t0 * P : t1 * P].bitcast(FP8X4),
-                    scales=wa_sc[:, t0 * P : t1 * P],
+                    out=wa_q[a][:, t0 * P : t1 * P].bitcast(FP8X4),
+                    scales=wa_sc[a][:, t0 * P : t1 * P],
                     in_=grouped[:, t0:t1].rearrange("p t m j -> p (t m j)"),
                 )
-            width = HALF // 2 if a == PASSES - 1 else HALF
-            for s in range(HALVES):
-                for lo in range(0, HALF, width):
-                    first = s * HALF + lo
-                    if a > 0:
-                        gather(a, s, lo, width)
-                    for t in range(PACK):
-                        nc.tensor.matmul_mx(
-                            out=h_banks[PACK * s + t][:, lo : lo + width],
-                            lhsT=wa_q[:, t * P : (t + 1) * P].bitcast(FP8X4),
-                            lhsT_scale=wa_sc[:, t * P : (t + 1) * P],
-                            rhs=v[a][s][:, lo : lo + width].bitcast(FP8X4),
-                            rhs_scale=v_sc[4 * a :, first : first + width],
-                            start=(a == 0),
-                            stop=(a == PASSES - 1 and lo + width == HALF),
-                        )
 
-        h_sum = []
+        def down(acc, a, s, t, start, stop):
+            nc.tensor.matmul_mx(
+                out=acc[:],
+                lhsT=wa_q[a][:, t * P : (t + 1) * P].bitcast(FP8X4),
+                lhsT_scale=wa_sc[a][:, t * P : (t + 1) * P],
+                rhs=v[a][s][:].bitcast(FP8X4),
+                rhs_scale=v_sc[4 * a :, s * HALF : (s + 1) * HALF],
+                start=start,
+                stop=stop,
+            )
+
+        def dense(acc, a, s, n):
+            part, col = (0, n * P) if n * P < EARLY_N else (1, n * P - EARLY_N)
+            cols = slice(s * HALF, (s + 1) * HALF)
+            nc.tensor.matmul_mx(
+                out=acc[:],
+                lhsT=wd[part][:, a, 2 * col : 2 * (col + P)].bitcast(FP4X4),
+                lhsT_scale=wd_sc[part][:, a, col : col + P],
+                rhs=v[a][s][:].bitcast(FP8X4),
+                rhs_scale=v_sc[:, cols] if a == 0 else v_sc_low[:, a - 1, cols],
+                start=(a == 0),
+                stop=False,
+            )
+
+        first = [[bank(PACK * s + t) for t in range(PACK)] for s in range(HALVES)]
+        quantize_wa(0, False)
         for s in range(HALVES):
-            h_sum.append(held([P, PACK, HALF], F32, "h_sum%d" % s))
             for t in range(PACK):
-                nc.scalar.activation(out=h_sum[s][:, t, :], in_=h_banks[PACK * s + t][:], func=COPY)
+                down(first[s][t], 0, s, t, True, False)
+        gather(1, 1)
+        quantize_wa(1, False)
+        for t in range(PACK):
+            down(first[1][t], 1, 1, t, False, True)
+        gather(1, 0)
+        for t in range(PACK):
+            down(first[0][t], 1, 0, t, False, False)
+        h_part = held([P, PACK, HALF], F32, "h_grouped0")
+        for t in range(PACK):
+            nc.scalar.activation(out=h_part[:, t, :], in_=first[1][t][:], func=COPY)
+
+        accs = {}
+        early = [(s, n) for s in range(HALVES) for n in range(EARLY_N // P)]
+        for i, tile in enumerate(early):
+            accs[tile] = bank(PACK + i)
+            for a in range(2):
+                dense(accs[tile], a, *tile)
+        for s in range(HALVES):
+            gather(2, s)
+        for tile in early:
+            dense(accs[tile], 2, *tile)
+        slots = (2, 3, 0, 1)
+        quantize_wa(2, True)
+        for t in slots:
+            down(first[0][t], 2, 0, t, False, False)
+        for s in range(HALVES):
+            gather(3, s)
+        for tile in early:
+            dense(accs[tile], 3, *tile)
+        quantize_wa(3, True)
+        h_sum = [held([P, PACK, HALF], F32, "h_sum%d" % s) for s in range(HALVES)]
+        for t in slots:
+            down(first[0][t], 3, 0, t, False, True)
+            if t != 3:
+                nc.scalar.activation(out=h_sum[0][:, t, :], in_=first[0][t][:], func=COPY)
+            else:
+                nc.vector.tensor_copy(out=h_sum[0][:, t, :], in_=first[0][t][:])
+        nc.vector.transpose(bias[:], bias_rows[:])
+        for t in slots:
+            second = bank(t)
+            down(second, 2, 1, t, True, False)
+            down(second, 3, 1, t, False, True)
+            nc.vector.tensor_tensor(out=h_sum[1][:, t, :], in0=second[:], in1=h_part[:, t, :], op=ADD)
+
+        def open_tile(tile, b):
+            accs[tile] = bank(b)
+            for a in range(PASSES):
+                dense(accs[tile], a, *tile)
+
+        for i, t in enumerate(slots):
+            open_tile((0, EARLY_N // P + i), t)
 
         def by_fours(ap, form):
             return ap.rearrange(form + " -> p c t i", i=PACK)
 
-        h_q, h_sc = [], []
+        h_grouped = []
+        h_q = [held([P, HALF], U32, "h_q%d" % s) for s in range(HALVES)]
+        h_sc = [held([P, HALF], U8, "h_sc%d" % s) for s in range(HALVES)]
+        wb_q = held([P, N], U32, "wb_q")
+        wb_sc = held([P, N], U8, "wb_sc")
 
-        def quantize_h(s):
-            h_grouped = held([P, HALF, PACK], BF16, "h_grouped%d" % s)
+        def weigh_h(s):
+            h_grouped.append(held([P, HALF, PACK], BF16, "h_grouped%d" % s))
             nc.vector.tensor_tensor(
-                out=by_fours(h_grouped[:], "p (c i) t"),
+                out=by_fours(h_grouped[s][:], "p (c i) t"),
                 in0=by_fours(h_sum[s][:], "p t (c i)"),
                 in1=by_fours(gains[s][:], "p t (c i)"),
                 op=MULT,
             )
-            h_q.append(held([P, HALF], U32, "h_q%d" % s))
-            h_sc.append(held([P, HALF], U8, "h_sc%d" % s))
+
+        def quantize_h(s):
             nc.vector.quantize_mx(
-                out=h_q[s][:].bitcast(FP8X4), scales=h_sc[s][:], in_=h_grouped[:].rearrange("p s t -> p (s t)")
+                out=h_q[s][:].bitcast(FP8X4), scales=h_sc[s][:], in_=h_grouped[s][:].rearrange("p s t -> p (s t)")
             )
 
-        quantize_h(0)
-        wb_q = held([P, N], U32, "wb_q")
-        wb_sc = held([P, N], U8, "wb_sc")
-        for lo in (0, 2 * WB_PART, WB_PART):
+        def quantize_wb(lo):
             hi = lo + WB_PART
-            wb_grouped = held([P, hi - lo, PACK], BF16, "wb_grouped%d" % lo)
-            dst = by_fours(wb_grouped[:], "p (c i) t")
-            src = by_fours(wb_raw[:, :, lo:hi], "p t (c i)")
-            if hi < N:
-                nc.vector.tensor_copy(out=dst, in_=src)
-            else:
-                nc.scalar.activation(out=dst, in_=src, func=COPY)
+            part, col = (0, lo) if lo < EARLY_N else (1, lo - EARLY_N)
+            wb_grouped = held([P, WB_PART, PACK], BF16, "wb_grouped%d" % lo)
+            nc.scalar.activation(
+                out=by_fours(wb_grouped[:], "p (c i) t"),
+                in_=by_fours(wb_raw[part][:, :, col : col + WB_PART], "p t (c i)"),
+                func=COPY,
+            )
             nc.vector.quantize_mx(
                 out=wb_q[:, lo:hi].bitcast(FP8X4),
                 scales=wb_sc[:, lo:hi],
                 in_=wb_grouped[:].rearrange("p n j -> p (n j)"),
             )
+
+        weigh_h(0)
+        quantize_wb(0)
+        quantize_h(0)
+        quantize_wb(WB_PART)
+        weigh_h(1)
+        quantize_wb(2 * WB_PART)
         quantize_h(1)
 
-        def dense(acc, s, n):
-            for a in range(PASSES):
-                cols = slice(s * HALF, (s + 1) * HALF)
-                nc.tensor.matmul_mx(
-                    out=acc[:],
-                    lhsT=wd[:, a, 2 * n * P : 2 * (n + 1) * P].bitcast(FP4X4),
-                    lhsT_scale=wd_sc[:, a, n * P : (n + 1) * P],
-                    rhs=v[a][s][:].bitcast(FP8X4),
-                    rhs_scale=v_sc[:, cols] if a == 0 else v_sc_low[:, a - 1, cols],
-                    start=(a == 0),
-                    stop=False,
-                )
-
-        def finish(acc, s, n):
+        def finish(s, n):
+            acc = accs[s, n]
             nc.tensor.matmul_mx(
                 out=acc[:],
                 lhsT=wb_q[:, n * P : (n + 1) * P].bitcast(FP8X4),
@@ -252,7 +315,7 @@ def tile_list_tenant_adapter_queries_kernel(
             for i in range(pieces):
                 result = stage.tile([P, width], F32, name="result")
                 sums = acc[:, i * width : (i + 1) * width]
-                if s == 1 and n in (1, 3):
+                if s == 1 and n in (0, 2, 4):
                     nc.vector.tensor_scalar(
                         out=result[:], in0=sums, scalar1=bias[:, 32 * n : 32 * n + 1], scalar2=None, op0=ADD
                     )
@@ -261,21 +324,14 @@ def tile_list_tenant_adapter_queries_kernel(
                 col = s * HALF + i * width
                 nc.sync.dma_start(out=out[n * P : (n + 1) * P, col : col + width], in_=result[:])
 
-        tiles = [(s, n) for s in range(HALVES) for n in range(N_TILES)]
-        accs = [bank(b) for b in range(BANKS)]
-        for i in range(BANKS - 1):
-            dense(accs[i], *tiles[i])
-        finish(accs[0], *tiles[0])
-        finish(accs[1], *tiles[1])
-        dense(accs[BANKS - 1], *tiles[BANKS - 1])
-        for i in range(2, N_TILES):
-            finish(accs[i], *tiles[i])
-        for i in (8, 9):
-            accs.append(bank(i - BANKS))
-            dense(accs[i], *tiles[i])
-        for i in range(N_TILES, 10):
-            finish(accs[i], *tiles[i])
-        for i, b in ((10, 2), (11, 6)):
-            accs.append(bank(b))
-            dense(accs[i], *tiles[i])
-            finish(accs[i], *tiles[i])
+        for n in range(4):
+            finish(0, n)
+        open_tile((1, 2), 4)
+        open_tile((1, 3), 5)
+        finish(0, 4)
+        finish(0, 5)
+        open_tile((1, 4), 2)
+        for n in range(5):
+            finish(1, n)
+        open_tile((1, 5), 6)
+        finish(1, 5)

@@ -57,7 +57,8 @@ def tile_list_tenant_adapter_queries_kernel(
         wa_raw = [held([P, PACK, R], F32, "wa_raw%d" % a) for a in range(PASSES)]
         tab = [held([P, T], I32, "tab%d" % a) for a in range(PASSES)]
         gains = [held([P, PACK, HALF], F32, "gain%d" % s) for s in range(HALVES)]
-        wb_raw = [held([P, PACK, hi - lo], F32, "wb_raw%d" % lo) for lo, hi in col_parts]
+        wb_parts = ((0, 2 * WB_PART), (2 * WB_PART, N))
+        wb_raw = [held([P, PACK, hi - lo], F32, "wb_raw%d" % lo) for lo, hi in wb_parts]
         v = [[held([P, HALF], U32, "v%d_%d" % (a, s)) for s in range(HALVES)] for a in range(PASSES)]
 
         def clear(words):
@@ -97,7 +98,7 @@ def tile_list_tenant_adapter_queries_kernel(
             )
 
         def load_wb(part):
-            lo, hi = col_parts[part]
+            lo, hi = wb_parts[part]
             nc.sync.dma_start(out=wb_raw[part][:], in_=wb[:, lo:hi].rearrange("(p j) n -> p j n", j=PACK))
 
         def load_gain(s):
@@ -113,22 +114,19 @@ def tile_list_tenant_adapter_queries_kernel(
             )
 
         nc.vector.memset(tab_sc[:].bitcast(I32), 0)
-        load_tab(0)
         nc.sync.dma_start(offsets[:], offs)
+        load_wa(0)
         load_tab_scales()
         clear(wd_sc[0][:].rearrange("p a n -> p (a n)").bitcast(I32))
-        load_wa(0)
+        load_tab(0)
         load_wa(1)
         load_wd_scales(0)
         load_tab(1)
         load_wd(0)
-        load_tab(2)
 
         clear(v_sc_low[:].rearrange("p a s -> p (a s)").bitcast(I32))
         clear(wd_sc[1][:].rearrange("p a n -> p (a n)").bitcast(I32))
 
-        for s in range(HALVES):
-            gather(0, s)
         nc.vector.tensor_copy(out=v_sc[:], in_=tab_sc[:].indirect(offsets[:]))
 
         for a in range(1, PASSES):
@@ -136,9 +134,11 @@ def tile_list_tenant_adapter_queries_kernel(
                 out=v_sc_low[0:SHIFT_ROWS, a - 1, :].bitcast(I32),
                 in_=v_sc[4 * a : 4 * a + SHIFT_ROWS, :].bitcast(I32),
             )
+        load_tab(2)
         load_wa(2)
         load_tab(3)
         load_wa(3)
+        load_gain(0)
         load_wd(1)
         load_wd_scales(1)
         bias_rows = held([P, 256], F32, "bias_rows")
@@ -149,9 +149,8 @@ def tile_list_tenant_adapter_queries_kernel(
             in_=bq.rearrange("(c q i) -> q c i", q=QUADS, i=32),
         )
         load_wb(0)
-        load_gain(0)
-        load_wb(1)
         load_gain(1)
+        load_wb(1)
 
         wa_q = [held([P, R], U32, "wa_q%d" % a) for a in range(PASSES)]
         wa_sc = [held([P, R], U8, "wa_sc%d" % a) for a in range(PASSES)]
@@ -165,7 +164,7 @@ def tile_list_tenant_adapter_queries_kernel(
                 nc.vector.tensor_copy(out=dst[:, :, :, 2:], in_=src[:, :, :, 2:])
             else:
                 nc.scalar.activation(out=dst[:, :, :, 2:], in_=src[:, :, :, 2:], func=COPY)
-            for t0, t1 in ((2, PACK), (0, 2)) if shared else ((0, PACK),):
+            for t0, t1 in ((2, PACK), (0, 2)) if shared else ((0, 2), (2, PACK)):
                 nc.vector.quantize_mx(
                     out=wa_q[a][:, t0 * P : t1 * P].bitcast(FP8X4),
                     scales=wa_sc[a][:, t0 * P : t1 * P],
@@ -199,16 +198,17 @@ def tile_list_tenant_adapter_queries_kernel(
         first = [[bank(PACK * s + t) for t in range(PACK)] for s in range(HALVES)]
         quantize_wa(0, False)
         for s in range(HALVES):
+            gather(0, s)
             for t in range(PACK):
                 down(first[s][t], 0, s, t, True, False)
+        quantize_wa(1, True)
         gather(1, 1)
-        quantize_wa(1, False)
         for t in range(PACK):
             down(first[1][t], 1, 1, t, False, True)
         gather(1, 0)
         for t in range(PACK):
             down(first[0][t], 1, 0, t, False, False)
-        h_part = held([P, PACK, HALF], F32, "h_grouped0")
+        h_part = held([P, PACK, HALF], F32, "h_part")
         for t in range(PACK):
             nc.scalar.activation(out=h_part[:, t, :], in_=first[1][t][:], func=COPY)
 
@@ -234,16 +234,17 @@ def tile_list_tenant_adapter_queries_kernel(
         h_sum = [held([P, PACK, HALF], F32, "h_sum%d" % s) for s in range(HALVES)]
         for t in slots:
             down(first[0][t], 3, 0, t, False, True)
-            if t != 3:
+            if t % 2 == 0:
                 nc.scalar.activation(out=h_sum[0][:, t, :], in_=first[0][t][:], func=COPY)
             else:
                 nc.vector.tensor_copy(out=h_sum[0][:, t, :], in_=first[0][t][:])
         nc.vector.transpose(bias[:], bias_rows[:])
+        h_rest = held([P, PACK, HALF], F32, "h_rest")
         for t in slots:
             second = bank(t)
             down(second, 2, 1, t, True, False)
             down(second, 3, 1, t, False, True)
-            nc.vector.tensor_tensor(out=h_sum[1][:, t, :], in0=second[:], in1=h_part[:, t, :], op=ADD)
+            nc.scalar.activation(out=h_rest[:, t, :], in_=second[:], func=COPY)
 
         def open_tile(tile, b):
             accs[tile] = bank(b)
@@ -278,13 +279,14 @@ def tile_list_tenant_adapter_queries_kernel(
 
         def quantize_wb(lo):
             hi = lo + WB_PART
-            part, col = (0, lo) if lo < EARLY_N else (1, lo - EARLY_N)
-            wb_grouped = held([P, WB_PART, PACK], BF16, "wb_grouped%d" % lo)
-            nc.scalar.activation(
-                out=by_fours(wb_grouped[:], "p (c i) t"),
-                in_=by_fours(wb_raw[part][:, :, col : col + WB_PART], "p t (c i)"),
-                func=COPY,
-            )
+            part, col = (0, lo) if hi < N else (1, 0)
+            wb_grouped = held([P, WB_PART, PACK], BF16, "wb_grouped%d" % lo if part == 0 else "h_grouped1")
+            dst = by_fours(wb_grouped[:], "p (c i) t")
+            src = by_fours(wb_raw[part][:, :, col : col + WB_PART], "p t (c i)")
+            if part == 0:
+                nc.scalar.activation(out=dst, in_=src, func=COPY)
+            else:
+                nc.vector.tensor_copy(out=dst, in_=src)
             nc.vector.quantize_mx(
                 out=wb_q[:, lo:hi].bitcast(FP8X4),
                 scales=wb_sc[:, lo:hi],
@@ -292,12 +294,13 @@ def tile_list_tenant_adapter_queries_kernel(
             )
 
         weigh_h(0)
-        quantize_wb(0)
         quantize_h(0)
+        nc.vector.tensor_tensor(out=h_sum[1][:], in0=h_rest[:], in1=h_part[:], op=ADD)
+        quantize_wb(0)
         quantize_wb(WB_PART)
         weigh_h(1)
-        quantize_wb(2 * WB_PART)
         quantize_h(1)
+        quantize_wb(2 * WB_PART)
 
         def finish(s, n):
             acc = accs[s, n]
@@ -315,7 +318,7 @@ def tile_list_tenant_adapter_queries_kernel(
             for i in range(pieces):
                 result = stage.tile([P, width], F32, name="result")
                 sums = acc[:, i * width : (i + 1) * width]
-                if s == 1 and n in (0, 2, 4):
+                if s == 0 and n >= 4:
                     nc.vector.tensor_scalar(
                         out=result[:], in0=sums, scalar1=bias[:, 32 * n : 32 * n + 1], scalar2=None, op0=ADD
                     )
@@ -328,10 +331,10 @@ def tile_list_tenant_adapter_queries_kernel(
             finish(0, n)
         open_tile((1, 2), 4)
         open_tile((1, 3), 5)
+        for n in range(4):
+            finish(1, n)
         finish(0, 4)
         finish(0, 5)
-        open_tile((1, 4), 2)
-        for n in range(5):
+        for n, b in ((4, 6), (5, 7)):
+            open_tile((1, n), b)
             finish(1, n)
-        open_tile((1, 5), 6)
-        finish(1, 5)

@@ -114,19 +114,22 @@ def tile_list_tenant_adapter_queries_kernel(
             )
 
         nc.vector.memset(tab_sc[:].bitcast(I32), 0)
+        load_tab(0)
         nc.sync.dma_start(offsets[:], offs)
-        load_wa(0)
         load_tab_scales()
         clear(wd_sc[0][:].rearrange("p a n -> p (a n)").bitcast(I32))
-        load_tab(0)
+        load_wa(0)
         load_wa(1)
         load_wd_scales(0)
         load_tab(1)
         load_wd(0)
+        load_tab(2)
 
         clear(v_sc_low[:].rearrange("p a s -> p (a s)").bitcast(I32))
         clear(wd_sc[1][:].rearrange("p a n -> p (a n)").bitcast(I32))
 
+        for s in range(HALVES):
+            gather(0, s)
         nc.vector.tensor_copy(out=v_sc[:], in_=tab_sc[:].indirect(offsets[:]))
 
         for a in range(1, PASSES):
@@ -134,11 +137,9 @@ def tile_list_tenant_adapter_queries_kernel(
                 out=v_sc_low[0:SHIFT_ROWS, a - 1, :].bitcast(I32),
                 in_=v_sc[4 * a : 4 * a + SHIFT_ROWS, :].bitcast(I32),
             )
-        load_tab(2)
         load_wa(2)
         load_tab(3)
         load_wa(3)
-        load_gain(0)
         load_wd(1)
         load_wd_scales(1)
         bias_rows = held([P, 256], F32, "bias_rows")
@@ -148,6 +149,7 @@ def tile_list_tenant_adapter_queries_kernel(
             out=bias_rows[0:P:32, 0 : 32 * N_TILES].rearrange("q (c i) -> q c i", i=32),
             in_=bq.rearrange("(c q i) -> q c i", q=QUADS, i=32),
         )
+        load_gain(0)
         load_wb(0)
         load_gain(1)
         load_wb(1)
@@ -198,11 +200,10 @@ def tile_list_tenant_adapter_queries_kernel(
         first = [[bank(PACK * s + t) for t in range(PACK)] for s in range(HALVES)]
         quantize_wa(0, False)
         for s in range(HALVES):
-            gather(0, s)
             for t in range(PACK):
                 down(first[s][t], 0, s, t, True, False)
-        quantize_wa(1, True)
         gather(1, 1)
+        quantize_wa(1, False)
         for t in range(PACK):
             down(first[1][t], 1, 1, t, False, True)
         gather(1, 0)

@@ -232,7 +232,7 @@ def tile_list_tenant_adapter_queries_kernel(
         for tile in early:
             dense(accs[tile], 3, *tile)
         quantize_wa(3, True)
-        h_sum = [held([P, PACK, HALF], F32, "h_sum%d" % s) for s in range(HALVES)]
+        h_sum = [held([P, PACK, HALF], F32, "h_sum")]
         for t in slots:
             down(first[0][t], 3, 0, t, False, True)
             if t % 2 == 0:
@@ -296,6 +296,7 @@ def tile_list_tenant_adapter_queries_kernel(
 
         weigh_h(0)
         quantize_h(0)
+        h_sum.append(held([P, PACK, HALF], F32, "h_sum"))
         nc.vector.tensor_tensor(out=h_sum[1][:], in0=h_rest[:], in1=h_part[:], op=ADD)
         quantize_wb(0)
         quantize_wb(WB_PART)

@@ -59,7 +59,7 @@ def tile_list_tenant_adapter_queries_kernel(
         gains = [held([P, PACK, HALF], F32, "gain%d" % s) for s in range(HALVES)]
         wb_parts = ((0, 2 * WB_PART), (2 * WB_PART, N))
         wb_raw = [held([P, PACK, hi - lo], F32, "wb_raw%d" % lo) for lo, hi in wb_parts]
-        v = [[held([P, HALF], U32, "v%d_%d" % (a, s)) for s in range(HALVES)] for a in range(PASSES)]
+        v = {}
 
         def clear(words):
             last = words.shape[1] - 1
@@ -107,9 +107,16 @@ def tile_list_tenant_adapter_queries_kernel(
                 in_=gain[:, s * HALF : (s + 1) * HALF].rearrange("(p j) s -> p j s", j=PACK),
             )
 
+        def gather_both(a):
+            both = held([P, S], U32, "v%d" % a)
+            nc.vector.tensor_copy(out=both[:], in_=tab[a][:].bitcast(U32).indirect(offsets[:]))
+            for s in range(HALVES):
+                v[a, s] = both[:, s * HALF : (s + 1) * HALF]
+
         def gather(a, s):
+            v[a, s] = held([P, HALF], U32, "v%d_%d" % (a, s))[:]
             nc.vector.tensor_copy(
-                out=v[a][s][:],
+                out=v[a, s],
                 in_=tab[a][:].bitcast(U32).indirect(offsets[:, s * HALF // 16 : (s + 1) * HALF // 16]),
             )
 
@@ -117,68 +124,70 @@ def tile_list_tenant_adapter_queries_kernel(
         load_tab(0)
         nc.sync.dma_start(offsets[:], offs)
         load_tab_scales()
+        bias_rows = held([P, 256], F32, "v0")
+        bias = held([P, 256], F32, "bias")
+        clear(bias_rows[:].bitcast(I32))
+        nc.scalar.dma_start(
+            out=bias_rows[0:P:32, 0 : 32 * N_TILES].rearrange("q (c i) -> q c i", i=32),
+            in_=bq.rearrange("(c q i) -> q c i", q=QUADS, i=32),
+        )
+        nc.vector.transpose(bias[:], bias_rows[:])
         clear(wd_sc[0][:].rearrange("p a n -> p (a n)").bitcast(I32))
         load_wa(0)
+        load_tab(1)
         load_wa(1)
         load_wd_scales(0)
-        load_tab(1)
         load_wd(0)
         load_tab(2)
 
         clear(v_sc_low[:].rearrange("p a s -> p (a s)").bitcast(I32))
         clear(wd_sc[1][:].rearrange("p a n -> p (a n)").bitcast(I32))
 
-        for s in range(HALVES):
-            gather(0, s)
-        nc.vector.tensor_copy(out=v_sc[:], in_=tab_sc[:].indirect(offsets[:]))
-
-        for a in range(1, PASSES):
+        def shift(a):
             nc.sync.dma_start(
                 out=v_sc_low[0:SHIFT_ROWS, a - 1, :].bitcast(I32),
                 in_=v_sc[4 * a : 4 * a + SHIFT_ROWS, :].bitcast(I32),
             )
-        load_wa(2)
-        load_tab(3)
-        load_wa(3)
-        load_wd(1)
-        load_wd_scales(1)
-        bias_rows = held([P, 256], F32, "bias_rows")
-        bias = held([P, 256], F32, "bias")
-        clear(bias_rows[:].bitcast(I32))
-        nc.sync.dma_start(
-            out=bias_rows[0:P:32, 0 : 32 * N_TILES].rearrange("q (c i) -> q c i", i=32),
-            in_=bq.rearrange("(c q i) -> q c i", q=QUADS, i=32),
-        )
-        load_gain(0)
-        load_wb(0)
-        load_gain(1)
-        load_wb(1)
+
+        def later_loads():
+            for a in range(1, PASSES):
+                shift(a)
+            load_tab(3)
+            load_wa(2)
+            load_wa(3)
+            load_wd(1)
+            load_wd_scales(1)
+            load_gain(0)
+            load_wb(0)
+            load_gain(1)
+            load_wb(1)
 
         wa_q = [held([P, R], U32, "wa_q%d" % a) for a in range(PASSES)]
         wa_sc = [held([P, R], U8, "wa_sc%d" % a) for a in range(PASSES)]
 
-        def quantize_wa(a, shared):
-            grouped = held([P, PACK, P, PACK], BF16, "wa_grouped%d" % a)
-            dst = grouped[:].rearrange("p t m j -> p m j t")
-            src = wa_raw[a][:].rearrange("p j (m t) -> p m j t", t=PACK)
-            nc.scalar.activation(out=dst[:, :, :, :2], in_=src[:, :, :, :2], func=COPY)
-            if shared:
-                nc.vector.tensor_copy(out=dst[:, :, :, 2:], in_=src[:, :, :, 2:])
+        def group_wa(a, t0, name, on_vector=False):
+            pair = held([P, 2, P, PACK], BF16, name)
+            dst = pair[:].rearrange("p t m j -> p m j t")
+            src = wa_raw[a][:].rearrange("p j (m t) -> p m j t", t=PACK)[:, :, :, t0 : t0 + 2]
+            if on_vector:
+                nc.vector.tensor_copy(out=dst, in_=src)
             else:
-                nc.scalar.activation(out=dst[:, :, :, 2:], in_=src[:, :, :, 2:], func=COPY)
-            for t0, t1 in ((2, PACK), (0, 2)) if shared else ((0, 2), (2, PACK)):
-                nc.vector.quantize_mx(
-                    out=wa_q[a][:, t0 * P : t1 * P].bitcast(FP8X4),
-                    scales=wa_sc[a][:, t0 * P : t1 * P],
-                    in_=grouped[:, t0:t1].rearrange("p t m j -> p (t m j)"),
-                )
+                nc.scalar.activation(out=dst, in_=src, func=COPY)
+            return pair
+
+        def quantize_wa(a, t0, pair):
+            nc.vector.quantize_mx(
+                out=wa_q[a][:, t0 * P : (t0 + 2) * P].bitcast(FP8X4),
+                scales=wa_sc[a][:, t0 * P : (t0 + 2) * P],
+                in_=pair[:].rearrange("p t m j -> p (t m j)"),
+            )
 
         def down(acc, a, s, t, start, stop):
             nc.tensor.matmul_mx(
                 out=acc[:],
                 lhsT=wa_q[a][:, t * P : (t + 1) * P].bitcast(FP8X4),
                 lhsT_scale=wa_sc[a][:, t * P : (t + 1) * P],
-                rhs=v[a][s][:].bitcast(FP8X4),
+                rhs=v[a, s].bitcast(FP8X4),
                 rhs_scale=v_sc[4 * a :, s * HALF : (s + 1) * HALF],
                 start=start,
                 stop=stop,
@@ -191,22 +200,29 @@ def tile_list_tenant_adapter_queries_kernel(
                 out=acc[:],
                 lhsT=wd[part][:, a, 2 * col : 2 * (col + P)].bitcast(FP4X4),
                 lhsT_scale=wd_sc[part][:, a, col : col + P],
-                rhs=v[a][s][:].bitcast(FP8X4),
+                rhs=v[a, s].bitcast(FP8X4),
                 rhs_scale=v_sc[:, cols] if a == 0 else v_sc_low[:, a - 1, cols],
                 start=(a == 0),
                 stop=False,
             )
 
         first = [[bank(PACK * s + t) for t in range(PACK)] for s in range(HALVES)]
-        quantize_wa(0, False)
+        gather_both(0)
+        nc.vector.tensor_copy(out=v_sc[:], in_=tab_sc[:].indirect(offsets[:]))
+        later_loads()
+        for t0 in (0, 2):
+            quantize_wa(0, t0, group_wa(0, t0, "wa_pair0_%d" % t0))
         for s in range(HALVES):
             for t in range(PACK):
                 down(first[s][t], 0, s, t, True, False)
         gather(1, 1)
-        quantize_wa(1, False)
-        for t in range(PACK):
+        quantize_wa(1, 0, group_wa(1, 0, "v1_0"))
+        for t in (0, 1):
             down(first[1][t], 1, 1, t, False, True)
         gather(1, 0)
+        quantize_wa(1, 2, group_wa(1, 2, "wa_pair1_2"))
+        for t in (2, 3):
+            down(first[1][t], 1, 1, t, False, True)
         for t in range(PACK):
             down(first[0][t], 1, 0, t, False, False)
         h_part = held([P, PACK, HALF], F32, "h_part")
@@ -219,33 +235,34 @@ def tile_list_tenant_adapter_queries_kernel(
             accs[tile] = bank(PACK + i)
             for a in range(2):
                 dense(accs[tile], a, *tile)
-        for s in range(HALVES):
-            gather(2, s)
+        gather_both(2)
         for tile in early:
             dense(accs[tile], 2, *tile)
-        slots = (2, 3, 0, 1)
-        quantize_wa(2, True)
-        for t in slots:
-            down(first[0][t], 2, 0, t, False, False)
-        for s in range(HALVES):
-            gather(3, s)
+        gather_both(3)
         for tile in early:
             dense(accs[tile], 3, *tile)
-        quantize_wa(3, True)
-        h_sum = [held([P, PACK, HALF], F32, "h_sum")]
+        slots = (2, 3, 0, 1)
+        for a in (2, 3):
+            low = group_wa(a, 0, "wa_pair%d_0" % a)
+            quantize_wa(a, 2, group_wa(a, 2, "wa_pair%d_2" % a, True))
+            quantize_wa(a, 0, low)
+            if a == 2:
+                for t in slots:
+                    down(first[0][t], 2, 0, t, False, False)
+        h_both = held([P, PACK + 2, HALF], F32, "h_both")
+        h_sum = [h_both[:, 0:PACK, :], h_both[:, 2:, :]]
         for t in slots:
             down(first[0][t], 3, 0, t, False, True)
-            if t % 2 == 0:
-                nc.scalar.activation(out=h_sum[0][:, t, :], in_=first[0][t][:], func=COPY)
-            else:
-                nc.vector.tensor_copy(out=h_sum[0][:, t, :], in_=first[0][t][:])
-        nc.vector.transpose(bias[:], bias_rows[:])
-        h_rest = held([P, PACK, HALF], F32, "h_rest")
+            nc.scalar.activation(out=h_sum[0][:, t, :], in_=first[0][t][:], func=COPY)
+        h_rest = held([P, 2, HALF], F32, "h_rest")
         for t in slots:
             second = bank(t)
             down(second, 2, 1, t, True, False)
             down(second, 3, 1, t, False, True)
-            nc.scalar.activation(out=h_rest[:, t, :], in_=second[:], func=COPY)
+            if t >= 2:
+                nc.vector.tensor_tensor(out=h_sum[1][:, t, :], in0=second[:], in1=h_part[:, t, :], op=ADD)
+            else:
+                nc.scalar.activation(out=h_rest[:, t, :], in_=second[:], func=COPY)
 
         def open_tile(tile, b):
             accs[tile] = bank(b)
@@ -268,7 +285,7 @@ def tile_list_tenant_adapter_queries_kernel(
             h_grouped.append(held([P, HALF, PACK], BF16, "h_grouped%d" % s))
             nc.vector.tensor_tensor(
                 out=by_fours(h_grouped[s][:], "p (c i) t"),
-                in0=by_fours(h_sum[s][:], "p t (c i)"),
+                in0=by_fours(h_sum[s], "p t (c i)"),
                 in1=by_fours(gains[s][:], "p t (c i)"),
                 op=MULT,
             )
@@ -281,7 +298,7 @@ def tile_list_tenant_adapter_queries_kernel(
         def quantize_wb(lo):
             hi = lo + WB_PART
             part, col = (0, lo) if hi < N else (1, 0)
-            wb_grouped = held([P, WB_PART, PACK], BF16, "wb_grouped%d" % lo if part == 0 else "h_grouped1")
+            wb_grouped = held([P, WB_PART, PACK], BF16, "wb_grouped0" if lo == 0 else "h_grouped1")
             dst = by_fours(wb_grouped[:], "p (c i) t")
             src = by_fours(wb_raw[part][:, :, col : col + WB_PART], "p t (c i)")
             if part == 0:
@@ -296,8 +313,7 @@ def tile_list_tenant_adapter_queries_kernel(
 
         weigh_h(0)
         quantize_h(0)
-        h_sum.append(held([P, PACK, HALF], F32, "h_sum"))
-        nc.vector.tensor_tensor(out=h_sum[1][:], in0=h_rest[:], in1=h_part[:], op=ADD)
+        nc.vector.tensor_tensor(out=h_sum[1][:, :2, :], in0=h_rest[:], in1=h_part[:, :2, :], op=ADD)
         quantize_wb(0)
         quantize_wb(WB_PART)
         weigh_h(1)

@@ -26,7 +26,7 @@ HALVES = S // HALF
 N_TILES = N // P
 QUADS = 4
 BANKS = 8
-SHIFT_ROWS = 112
+SHIFT_ROWS = 100
 WB_PART = 256
 EARLY_N = 256
 
@@ -124,14 +124,12 @@ def tile_list_tenant_adapter_queries_kernel(
         load_tab(0)
         nc.sync.dma_start(offsets[:], offs)
         load_tab_scales()
-        bias_rows = held([P, 256], F32, "v0")
-        bias = held([P, 256], F32, "bias")
+        bias_rows = held([P, 256], F32, "bias_rows")
         clear(bias_rows[:].bitcast(I32))
         nc.scalar.dma_start(
             out=bias_rows[0:P:32, 0 : 32 * N_TILES].rearrange("q (c i) -> q c i", i=32),
             in_=bq.rearrange("(c q i) -> q c i", q=QUADS, i=32),
         )
-        nc.vector.transpose(bias[:], bias_rows[:])
         clear(wd_sc[0][:].rearrange("p a n -> p (a n)").bitcast(I32))
         load_wa(0)
         load_tab(1)
@@ -210,8 +208,8 @@ def tile_list_tenant_adapter_queries_kernel(
         gather_both(0)
         nc.vector.tensor_copy(out=v_sc[:], in_=tab_sc[:].indirect(offsets[:]))
         later_loads()
-        for t0 in (0, 2):
-            quantize_wa(0, t0, group_wa(0, t0, "wa_pair0_%d" % t0))
+        quantize_wa(0, 0, group_wa(0, 0, "wa_pair0_0"))
+        quantize_wa(0, 2, group_wa(0, 2, "v1_1"))
         for s in range(HALVES):
             for t in range(PACK):
                 down(first[s][t], 0, s, t, True, False)
@@ -238,7 +236,8 @@ def tile_list_tenant_adapter_queries_kernel(
         gather_both(2)
         for tile in early:
             dense(accs[tile], 2, *tile)
-        gather_both(3)
+        for s in range(HALVES):
+            gather(3, s)
         for tile in early:
             dense(accs[tile], 3, *tile)
         slots = (2, 3, 0, 1)
@@ -249,6 +248,8 @@ def tile_list_tenant_adapter_queries_kernel(
             if a == 2:
                 for t in slots:
                     down(first[0][t], 2, 0, t, False, False)
+        bias = held([P, 256], F32, "wa_pair3_0")
+        nc.vector.transpose(bias[:], bias_rows[:])
         h_both = held([P, PACK + 2, HALF], F32, "h_both")
         h_sum = [h_both[:, 0:PACK, :], h_both[:, 2:, :]]
         for t in slots:
@@ -278,7 +279,7 @@ def tile_list_tenant_adapter_queries_kernel(
         h_grouped = []
         h_q = [held([P, HALF], U32, "h_q%d" % s) for s in range(HALVES)]
         h_sc = [held([P, HALF], U8, "h_sc%d" % s) for s in range(HALVES)]
-        wb_q = held([P, N], U32, "wb_q")
+        wb_q = []
         wb_sc = held([P, N], U8, "wb_sc")
 
         def weigh_h(s):
@@ -295,19 +296,19 @@ def tile_list_tenant_adapter_queries_kernel(
                 out=h_q[s][:].bitcast(FP8X4), scales=h_sc[s][:], in_=h_grouped[s][:].rearrange("p s t -> p (s t)")
             )
 
-        def quantize_wb(lo):
-            hi = lo + WB_PART
-            part, col = (0, lo) if hi < N else (1, 0)
-            wb_grouped = held([P, WB_PART, PACK], BF16, "wb_grouped0" if lo == 0 else "h_grouped1")
-            dst = by_fours(wb_grouped[:], "p (c i) t")
-            src = by_fours(wb_raw[part][:, :, col : col + WB_PART], "p t (c i)")
-            if part == 0:
-                nc.scalar.activation(out=dst, in_=src, func=COPY)
-            else:
-                nc.vector.tensor_copy(out=dst, in_=src)
+        def quantize_wb(part):
+            lo = part * WB_PART
+            raw, col = (wb_raw[0], lo) if lo + WB_PART < N else (wb_raw[1], 0)
+            wb_grouped = held([P, WB_PART, PACK], BF16, "h_grouped1" if part == 1 else "wb_grouped%d" % part)
+            nc.scalar.activation(
+                out=by_fours(wb_grouped[:], "p (c i) t"),
+                in_=by_fours(raw[:, :, col : col + WB_PART], "p t (c i)"),
+                func=COPY,
+            )
+            wb_q.append(held([P, WB_PART], U32, "h_grouped1" if part == 2 else "wb_q%d" % part))
             nc.vector.quantize_mx(
-                out=wb_q[:, lo:hi].bitcast(FP8X4),
-                scales=wb_sc[:, lo:hi],
+                out=wb_q[part][:].bitcast(FP8X4),
+                scales=wb_sc[:, lo : lo + WB_PART],
                 in_=wb_grouped[:].rearrange("p n j -> p (n j)"),
             )
 
@@ -315,16 +316,16 @@ def tile_list_tenant_adapter_queries_kernel(
         quantize_h(0)
         nc.vector.tensor_tensor(out=h_sum[1][:, :2, :], in0=h_rest[:], in1=h_part[:, :2, :], op=ADD)
         quantize_wb(0)
-        quantize_wb(WB_PART)
+        quantize_wb(1)
         weigh_h(1)
         quantize_h(1)
-        quantize_wb(2 * WB_PART)
+        quantize_wb(2)
 
         def finish(s, n):
             acc = accs[s, n]
             nc.tensor.matmul_mx(
                 out=acc[:],
-                lhsT=wb_q[:, n * P : (n + 1) * P].bitcast(FP8X4),
+                lhsT=wb_q[n // 2][:, n % 2 * P : (n % 2 + 1) * P].bitcast(FP8X4),
                 lhsT_scale=wb_sc[:, n * P : (n + 1) * P],
                 rhs=h_q[s][:].bitcast(FP8X4),
                 rhs_scale=h_sc[s][:],

@@ -26,7 +26,7 @@ HALVES = S // HALF
 N_TILES = N // P
 QUADS = 4
 BANKS = 8
-SHIFT_ROWS = 100
+SCALE_ROW0 = 32
 WB_PART = 256
 EARLY_N = 256
 
@@ -40,8 +40,8 @@ def tile_list_tenant_adapter_queries_kernel(
         stage = ctx.enter_context(tc.tile_pool(name="stage", bufs=13))
         psum = ctx.enter_context(tc.psum_pool(name="psum", bufs=1))
 
-        def held(shape, dtype, name):
-            return keep.tile(shape, dtype, name=name, align_bytes=64)
+        def held(shape, dtype, name, pool=keep):
+            return pool.tile(shape, dtype, name=name, align_bytes=64)
 
         def bank(b):
             return psum.tile([P, HALF], F32, name="bank%d" % b)
@@ -49,29 +49,15 @@ def tile_list_tenant_adapter_queries_kernel(
         offsets = keep.tile([P, S // 16], U16, name="offsets")
 
         col_parts = ((0, EARLY_N), (EARLY_N, N))
-        tab_sc = held([P, T], U8, "tab_sc")
-        wd_sc = [held([P, PASSES, hi - lo], U8, "wd_sc%d" % lo) for lo, hi in col_parts]
-        wd = [held([P, PASSES, 2 * (hi - lo)], U8, "wd%d" % lo) for lo, hi in col_parts]
-        v_sc = held([P, S], U8, "v_sc")
-        v_sc_low = held([P, PASSES - 1, S], U8, "v_sc_low")
-        wa_raw = [held([P, PACK, R], F32, "wa_raw%d" % a) for a in range(PASSES)]
-        tab = [held([P, T], I32, "tab%d" % a) for a in range(PASSES)]
-        gains = [held([P, PACK, HALF], F32, "gain%d" % s) for s in range(HALVES)]
+        v_rows = held([P, S], U8, "v_rows")
+        v_sc = held([P, PASSES, S], U8, "v_sc")
+        wa_raw = [held([P, PACK, R], F32, "wa_raw0")]
+        tab = [held([P, T], I32, "tab%d" % a) for a in range(2)]
         wb_parts = ((0, 2 * WB_PART), (2 * WB_PART, N))
-        wb_raw = [held([P, PACK, hi - lo], F32, "wb_raw%d" % lo) for lo, hi in wb_parts]
         v = {}
 
         def clear(words):
-            last = words.shape[1] - 1
-            nc.vector.memset(words[:, :last], 0)
-            nc.vector.memset(words[:, last:], 0)
-
-        def load_tab_scales():
-            for q in range(QUADS):
-                nc.gpsimd.dma_start(
-                    out=tab_sc[32 * q : 32 * q + 16, :].bitcast(I32),
-                    in_=tab_scales[:, 4 * q : 4 * q + 4, :].bitcast(I32),
-                )
+            nc.vector.memset(words, 0)
 
         def load_wa(a):
             nc.sync.dma_start(
@@ -82,10 +68,10 @@ def tile_list_tenant_adapter_queries_kernel(
         def load_tab(a):
             nc.sync.dma_start(out=tab[a][:], in_=tab_words[a].rearrange("p t i -> p (t i)").bitcast(I32))
 
-        def load_wd_scales(part):
+        def load_wd_scales(part, queue):
             lo, hi = col_parts[part]
             for r in range(4):
-                nc.sync.dma_start(
+                queue.dma_start(
                     out=wd_sc[part][r:P:32, :, :].bitcast(I32),
                     in_=wd_scales[:, r:16:4, lo:hi].rearrange("a q n -> q a n").bitcast(I32),
                 )
@@ -120,45 +106,55 @@ def tile_list_tenant_adapter_queries_kernel(
                 in_=tab[a][:].bitcast(U32).indirect(offsets[:, s * HALF // 16 : (s + 1) * HALF // 16]),
             )
 
-        nc.vector.memset(tab_sc[:].bitcast(I32), 0)
-        load_tab(0)
-        nc.sync.dma_start(offsets[:], offs)
-        load_tab_scales()
-        bias_rows = held([P, 256], F32, "bias_rows")
-        clear(bias_rows[:].bitcast(I32))
-        nc.scalar.dma_start(
-            out=bias_rows[0:P:32, 0 : 32 * N_TILES].rearrange("q (c i) -> q c i", i=32),
-            in_=bq.rearrange("(c q i) -> q c i", q=QUADS, i=32),
-        )
-        clear(wd_sc[0][:].rearrange("p a n -> p (a n)").bitcast(I32))
-        load_wa(0)
-        load_tab(1)
-        load_wa(1)
-        load_wd_scales(0)
-        load_wd(0)
-        load_tab(2)
-
-        clear(v_sc_low[:].rearrange("p a s -> p (a s)").bitcast(I32))
-        clear(wd_sc[1][:].rearrange("p a n -> p (a n)").bitcast(I32))
-
-        def shift(a):
+        with tc.tile_pool(name="window", bufs=1) as window:
+            tab_sc = held([P, T], U8, "tab_sc", window)
+            nc.sync.dma_start(offsets[:], offs)
             nc.sync.dma_start(
-                out=v_sc_low[0:SHIFT_ROWS, a - 1, :].bitcast(I32),
-                in_=v_sc[4 * a : 4 * a + SHIFT_ROWS, :].bitcast(I32),
+                out=tab_sc[SCALE_ROW0 : SCALE_ROW0 + 64, :].bitcast(I32),
+                in_=tab_scales.rearrange("a s t -> s a t").bitcast(I32),
             )
+            load_tab(0)
+            load_wa(0)
+            load_tab(1)
+            clear(tab_sc[:SCALE_ROW0, :].bitcast(I32))
+            clear(tab_sc[SCALE_ROW0 + 64 :, :].bitcast(I32))
+            clear(v_sc[:].rearrange("p a s -> p (a s)").bitcast(I32))
+            bias_rows = held([P, 256], F32, "bias_rows")
+            clear(bias_rows[:].bitcast(I32))
+            nc.sync.dma_start(
+                out=bias_rows[0:P:32, 0 : 32 * N_TILES].rearrange("q (c i) -> q c i", i=32),
+                in_=bq.rearrange("(c q i) -> q c i", q=QUADS, i=32),
+            )
+            nc.vector.tensor_copy(out=v_rows[:], in_=tab_sc[:].indirect(offsets[:]))
 
-        def later_loads():
-            for a in range(1, PASSES):
-                shift(a)
-            load_tab(3)
-            load_wa(2)
-            load_wa(3)
-            load_wd(1)
-            load_wd_scales(1)
-            load_gain(0)
-            load_wb(0)
-            load_gain(1)
-            load_wb(1)
+        later = ctx.enter_context(tc.tile_pool(name="later", bufs=1))
+        wa_raw.extend(held([P, PACK, R], F32, "wa_raw%d" % a, later) for a in range(1, PASSES))
+        tab.extend(held([P, T], I32, "tab%d" % a, later) for a in range(2, PASSES))
+        wd = [held([P, PASSES, 2 * (hi - lo)], U8, "wd%d" % lo, later) for lo, hi in col_parts]
+        wd_sc = [held([P, PASSES, hi - lo], U8, "wd_sc%d" % lo, later) for lo, hi in col_parts]
+        gains = [held([P, PACK, HALF], F32, "gain%d" % s, later) for s in range(HALVES)]
+        wb_raw = [held([P, PACK, hi - lo], F32, "wb_raw%d" % lo, later) for lo, hi in wb_parts]
+
+        for q in (0, 2, 1, 3):
+            nc.sync.dma_start(
+                out=v_sc[32 * q : 32 * q + 4, :, :].bitcast(I32),
+                in_=v_rows[SCALE_ROW0 + 16 * q : SCALE_ROW0 + 16 * (q + 1), :].bitcast(I32),
+            )
+        load_wa(1)
+        load_tab(2)
+        clear(wd_sc[0][:].rearrange("p a n -> p (a n)").bitcast(I32))
+        load_wd_scales(0, nc.sync)
+        load_wd(0)
+        load_tab(3)
+        load_wa(2)
+        load_wa(3)
+        load_wd(1)
+        clear(wd_sc[1][:].rearrange("p a n -> p (a n)").bitcast(I32))
+        load_wd_scales(1, nc.sync)
+        load_gain(0)
+        load_wb(0)
+        load_gain(1)
+        load_wb(1)
 
         wa_q = [held([P, R], U32, "wa_q%d" % a) for a in range(PASSES)]
         wa_sc = [held([P, R], U8, "wa_sc%d" % a) for a in range(PASSES)]
@@ -186,7 +182,7 @@ def tile_list_tenant_adapter_queries_kernel(
                 lhsT=wa_q[a][:, t * P : (t + 1) * P].bitcast(FP8X4),
                 lhsT_scale=wa_sc[a][:, t * P : (t + 1) * P],
                 rhs=v[a, s].bitcast(FP8X4),
-                rhs_scale=v_sc[4 * a :, s * HALF : (s + 1) * HALF],
+                rhs_scale=v_sc[:, a, s * HALF : (s + 1) * HALF],
                 start=start,
                 stop=stop,
             )
@@ -199,38 +195,37 @@ def tile_list_tenant_adapter_queries_kernel(
                 lhsT=wd[part][:, a, 2 * col : 2 * (col + P)].bitcast(FP4X4),
                 lhsT_scale=wd_sc[part][:, a, col : col + P],
                 rhs=v[a, s].bitcast(FP8X4),
-                rhs_scale=v_sc[:, cols] if a == 0 else v_sc_low[:, a - 1, cols],
+                rhs_scale=v_sc[:, a, cols],
                 start=(a == 0),
                 stop=False,
             )
 
         first = [[bank(PACK * s + t) for t in range(PACK)] for s in range(HALVES)]
+        slots = (2, 3, 0, 1)
         gather_both(0)
-        nc.vector.tensor_copy(out=v_sc[:], in_=tab_sc[:].indirect(offsets[:]))
-        later_loads()
         quantize_wa(0, 0, group_wa(0, 0, "wa_pair0_0"))
-        quantize_wa(0, 2, group_wa(0, 2, "v1_1"))
-        for s in range(HALVES):
-            for t in range(PACK):
+        quantize_wa(0, 2, group_wa(0, 2, "v1"))
+        for t in range(PACK):
+            for s in range(HALVES):
                 down(first[s][t], 0, s, t, True, False)
-        gather(1, 1)
-        quantize_wa(1, 0, group_wa(1, 0, "v1_0"))
-        for t in (0, 1):
+        gather_both(1)
+        low = group_wa(1, 0, "wa_pair1_0")
+        quantize_wa(1, 2, group_wa(1, 2, "wa_pair1_2", True))
+        quantize_wa(1, 0, low)
+        for t in slots:
             down(first[1][t], 1, 1, t, False, True)
-        gather(1, 0)
-        quantize_wa(1, 2, group_wa(1, 2, "wa_pair1_2"))
-        for t in (2, 3):
-            down(first[1][t], 1, 1, t, False, True)
-        for t in range(PACK):
+        for t in slots:
             down(first[0][t], 1, 0, t, False, False)
+        bias = held([P, 256], F32, "bias")
+        nc.vector.transpose(bias[:], bias_rows[:])
         h_part = held([P, PACK, HALF], F32, "h_part")
-        for t in range(PACK):
+        for t in slots:
             nc.scalar.activation(out=h_part[:, t, :], in_=first[1][t][:], func=COPY)
 
         accs = {}
         early = [(s, n) for s in range(HALVES) for n in range(EARLY_N // P)]
         for i, tile in enumerate(early):
-            accs[tile] = bank(PACK + i)
+            accs[tile] = bank(PACK + slots[i])
             for a in range(2):
                 dense(accs[tile], a, *tile)
         gather_both(2)
@@ -240,7 +235,6 @@ def tile_list_tenant_adapter_queries_kernel(
             gather(3, s)
         for tile in early:
             dense(accs[tile], 3, *tile)
-        slots = (2, 3, 0, 1)
         for a in (2, 3):
             low = group_wa(a, 0, "wa_pair%d_0" % a)
             quantize_wa(a, 2, group_wa(a, 2, "wa_pair%d_2" % a, True))
@@ -248,8 +242,6 @@ def tile_list_tenant_adapter_queries_kernel(
             if a == 2:
                 for t in slots:
                     down(first[0][t], 2, 0, t, False, False)
-        bias = held([P, 256], F32, "wa_pair3_0")
-        nc.vector.transpose(bias[:], bias_rows[:])
         h_both = held([P, PACK + 2, HALF], F32, "h_both")
         h_sum = [h_both[:, 0:PACK, :], h_both[:, 2:, :]]
         for t in slots:
@@ -348,12 +340,12 @@ def tile_list_tenant_adapter_queries_kernel(
 
         for n in range(4):
             finish(0, n)
-        open_tile((1, 2), 4)
-        open_tile((1, 3), 5)
+        open_tile((1, 2), 6)
+        open_tile((1, 3), 7)
         for n in range(4):
             finish(1, n)
         finish(0, 4)
         finish(0, 5)
-        for n, b in ((4, 6), (5, 7)):
+        for n, b in ((4, 4), (5, 5)):
             open_tile((1, n), b)
             finish(1, n)

@@ -131,7 +131,7 @@ def tile_list_tenant_adapter_queries_kernel(
         wa_raw.extend(held([P, PACK, R], F32, "wa_raw%d" % a, later) for a in range(1, PASSES))
         tab.extend(held([P, T], I32, "tab%d" % a, later) for a in range(2, PASSES))
         wd = [held([P, PASSES, 2 * (hi - lo)], U8, "wd%d" % lo, later) for lo, hi in col_parts]
-        wd_sc = [held([P, PASSES, hi - lo], U8, "wd_sc%d" % lo, later) for lo, hi in col_parts]
+        wd_sc = [held([P, PASSES, EARLY_N], U8, "wd_sc0", later)]
         gains = [held([P, PACK, HALF], F32, "gain%d" % s, later) for s in range(HALVES)]
         wb_raw = [held([P, PACK, hi - lo], F32, "wb_raw%d" % lo, later) for lo, hi in wb_parts]
 
@@ -148,13 +148,6 @@ def tile_list_tenant_adapter_queries_kernel(
         load_tab(3)
         load_wa(2)
         load_wa(3)
-        load_wd(1)
-        clear(wd_sc[1][:].rearrange("p a n -> p (a n)").bitcast(I32))
-        load_wd_scales(1, nc.sync)
-        load_gain(0)
-        load_wb(0)
-        load_gain(1)
-        load_wb(1)
 
         wa_q = [held([P, R], U32, "wa_q%d" % a) for a in range(PASSES)]
         wa_sc = [held([P, R], U8, "wa_sc%d" % a) for a in range(PASSES)]
@@ -203,8 +196,8 @@ def tile_list_tenant_adapter_queries_kernel(
         first = [[bank(PACK * s + t) for t in range(PACK)] for s in range(HALVES)]
         slots = (2, 3, 0, 1)
         gather_both(0)
-        quantize_wa(0, 0, group_wa(0, 0, "wa_pair0_0"))
-        quantize_wa(0, 2, group_wa(0, 2, "v1"))
+        quantize_wa(0, 0, group_wa(0, 0, "v1"))
+        quantize_wa(0, 2, group_wa(0, 2, "wa_pair0_2"))
         for t in range(PACK):
             for s in range(HALVES):
                 down(first[s][t], 0, s, t, True, False)
@@ -212,12 +205,18 @@ def tile_list_tenant_adapter_queries_kernel(
         low = group_wa(1, 0, "wa_pair1_0")
         quantize_wa(1, 2, group_wa(1, 2, "wa_pair1_2", True))
         quantize_wa(1, 0, low)
+        load_wd(1)
+        wd_sc.append(held([P, PASSES, N - EARLY_N], U8, "wa_raw1", later))
+        clear(wd_sc[1][:].rearrange("p a n -> p (a n)").bitcast(I32))
+        load_wd_scales(1, nc.sync)
+        load_gain(0)
+        load_wb(0)
+        load_gain(1)
+        load_wb(1)
         for t in slots:
             down(first[1][t], 1, 1, t, False, True)
         for t in slots:
             down(first[0][t], 1, 0, t, False, False)
-        bias = held([P, 256], F32, "bias")
-        nc.vector.transpose(bias[:], bias_rows[:])
         h_part = held([P, PACK, HALF], F32, "h_part")
         for t in slots:
             nc.scalar.activation(out=h_part[:, t, :], in_=first[1][t][:], func=COPY)
@@ -242,6 +241,8 @@ def tile_list_tenant_adapter_queries_kernel(
             if a == 2:
                 for t in slots:
                     down(first[0][t], 2, 0, t, False, False)
+        bias = held([P, 256], F32, "wa_pair3_0")
+        nc.vector.transpose(bias[:], bias_rows[:])
         h_both = held([P, PACK + 2, HALF], F32, "h_both")
         h_sum = [h_both[:, 0:PACK, :], h_both[:, 2:, :]]
         for t in slots:

@@ -22,13 +22,13 @@ P = 128
 PACK = 4
 PASSES = K // (P * PACK)
 HALF = 512
-HALVES = S // HALF
+QUARTER = 256
 N_TILES = N // P
 QUADS = 4
-BANKS = 8
 SCALE_ROW0 = 32
 WB_PART = 256
 EARLY_N = 256
+SLOTS = (2, 3, 0, 1)
 
 
 def tile_list_tenant_adapter_queries_kernel(
@@ -46,64 +46,43 @@ def tile_list_tenant_adapter_queries_kernel(
         def bank(b):
             return psum.tile([P, HALF], F32, name="bank%d" % b)
 
-        offsets = keep.tile([P, S // 16], U16, name="offsets")
+        def clear(words):
+            nc.vector.memset(words, 0)
 
-        col_parts = ((0, EARLY_N), (EARLY_N, N))
+        def rows_by_four(x, lo, hi):
+            return x[:, lo:hi].rearrange("(p j) c -> p j c", j=PACK)
+
+        def by_fours(ap, form):
+            return ap.rearrange(form + " -> p c t i", i=PACK)
+
+        offsets = keep.tile([P, S // 16], U16, name="offsets")
         v_rows = held([P, S], U8, "v_rows")
         v_sc = held([P, PASSES, S], U8, "v_sc")
         wa_raw = [held([P, PACK, R], F32, "wa_raw0")]
         tab = [held([P, T], I32, "tab%d" % a) for a in range(2)]
-        wb_parts = ((0, 2 * WB_PART), (2 * WB_PART, N))
-        v = {}
-
-        def clear(words):
-            nc.vector.memset(words, 0)
+        wd_cols = ((0, EARLY_N), (EARLY_N, N))
+        wb_cols = ((0, 2 * WB_PART), (2 * WB_PART, N))
+        gain_cols = ((0, HALF), (HALF, HALF + QUARTER), (HALF + QUARTER, S))
 
         def load_wa(a):
-            nc.sync.dma_start(
-                out=wa_raw[a][:],
-                in_=wa[a * P * PACK : (a + 1) * P * PACK, :].rearrange("(p j) c -> p j c", j=PACK),
-            )
+            nc.sync.dma_start(out=wa_raw[a][:], in_=rows_by_four(wa[a * P * PACK : (a + 1) * P * PACK, :], 0, R))
 
         def load_tab(a):
             nc.sync.dma_start(out=tab[a][:], in_=tab_words[a].rearrange("p t i -> p (t i)").bitcast(I32))
 
-        def load_wd_scales(part, queue):
-            lo, hi = col_parts[part]
+        def load_wd_scales(part):
+            lo, hi = wd_cols[part]
             for r in range(4):
-                queue.dma_start(
+                nc.sync.dma_start(
                     out=wd_sc[part][r:P:32, :, :].bitcast(I32),
                     in_=wd_scales[:, r:16:4, lo:hi].rearrange("a q n -> q a n").bitcast(I32),
                 )
 
         def load_wd(part):
-            lo, hi = col_parts[part]
+            lo, hi = wd_cols[part]
             nc.sync.dma_start(
                 out=wd[part][:].bitcast(I32),
                 in_=wd_words[:, :, 2 * lo : 2 * hi].rearrange("a p c -> p a c").bitcast(I32),
-            )
-
-        def load_wb(part):
-            lo, hi = wb_parts[part]
-            nc.sync.dma_start(out=wb_raw[part][:], in_=wb[:, lo:hi].rearrange("(p j) n -> p j n", j=PACK))
-
-        def load_gain(s):
-            nc.sync.dma_start(
-                out=gains[s][:],
-                in_=gain[:, s * HALF : (s + 1) * HALF].rearrange("(p j) s -> p j s", j=PACK),
-            )
-
-        def gather_both(a):
-            both = held([P, S], U32, "v%d" % a)
-            nc.vector.tensor_copy(out=both[:], in_=tab[a][:].bitcast(U32).indirect(offsets[:]))
-            for s in range(HALVES):
-                v[a, s] = both[:, s * HALF : (s + 1) * HALF]
-
-        def gather(a, s):
-            v[a, s] = held([P, HALF], U32, "v%d_%d" % (a, s))[:]
-            nc.vector.tensor_copy(
-                out=v[a, s],
-                in_=tab[a][:].bitcast(U32).indirect(offsets[:, s * HALF // 16 : (s + 1) * HALF // 16]),
             )
 
         with tc.tile_pool(name="window", bufs=1) as window:
@@ -119,21 +98,16 @@ def tile_list_tenant_adapter_queries_kernel(
             clear(tab_sc[:SCALE_ROW0, :].bitcast(I32))
             clear(tab_sc[SCALE_ROW0 + 64 :, :].bitcast(I32))
             clear(v_sc[:].rearrange("p a s -> p (a s)").bitcast(I32))
-            bias_rows = held([P, 256], F32, "bias_rows")
-            clear(bias_rows[:].bitcast(I32))
-            nc.sync.dma_start(
-                out=bias_rows[0:P:32, 0 : 32 * N_TILES].rearrange("q (c i) -> q c i", i=32),
-                in_=bq.rearrange("(c q i) -> q c i", q=QUADS, i=32),
-            )
             nc.vector.tensor_copy(out=v_rows[:], in_=tab_sc[:].indirect(offsets[:]))
 
         later = ctx.enter_context(tc.tile_pool(name="later", bufs=1))
         wa_raw.extend(held([P, PACK, R], F32, "wa_raw%d" % a, later) for a in range(1, PASSES))
         tab.extend(held([P, T], I32, "tab%d" % a, later) for a in range(2, PASSES))
-        wd = [held([P, PASSES, 2 * (hi - lo)], U8, "wd%d" % lo, later) for lo, hi in col_parts]
+        wd = [held([P, PASSES, 2 * (hi - lo)], U8, "wd%d" % lo, later) for lo, hi in wd_cols]
         wd_sc = [held([P, PASSES, EARLY_N], U8, "wd_sc0", later)]
-        gains = [held([P, PACK, HALF], F32, "gain%d" % s, later) for s in range(HALVES)]
-        wb_raw = [held([P, PACK, hi - lo], F32, "wb_raw%d" % lo, later) for lo, hi in wb_parts]
+        gains = [held([P, PACK, hi - lo], F32, "gain%d" % lo, later) for lo, hi in gain_cols]
+        wb_raw = [held([P, PACK, hi - lo], F32, "wb_raw%d" % lo, later) for lo, hi in wb_cols]
+        bias_rows = held([P, 256], F32, "bias_rows", later)
 
         for q in (0, 2, 1, 3):
             nc.sync.dma_start(
@@ -143,14 +117,33 @@ def tile_list_tenant_adapter_queries_kernel(
         load_wa(1)
         load_tab(2)
         clear(wd_sc[0][:].rearrange("p a n -> p (a n)").bitcast(I32))
-        load_wd_scales(0, nc.sync)
+        clear(bias_rows[:].bitcast(I32))
+        load_wd_scales(0)
         load_wd(0)
         load_tab(3)
         load_wa(2)
         load_wa(3)
+        nc.sync.dma_start(
+            out=bias_rows[0:P:32, 0 : 32 * N_TILES].rearrange("q (c i) -> q c i", i=32),
+            in_=bq.rearrange("(c q i) -> q c i", q=QUADS, i=32),
+        )
 
+        v = {}
         wa_q = [held([P, R], U32, "wa_q%d" % a) for a in range(PASSES)]
         wa_sc = [held([P, R], U8, "wa_sc%d" % a) for a in range(PASSES)]
+
+        def gather_both(a):
+            both = held([P, S], U32, "v%d" % a)
+            nc.vector.tensor_copy(out=both[:], in_=tab[a][:].bitcast(U32).indirect(offsets[:]))
+            for s in range(2):
+                v[a, s] = both[:, s * HALF : (s + 1) * HALF]
+
+        def gather_half(a, s):
+            v[a, s] = held([P, HALF], U32, "v%d_%d" % (a, s))[:]
+            nc.vector.tensor_copy(
+                out=v[a, s],
+                in_=tab[a][:].bitcast(U32).indirect(offsets[:, s * HALF // 16 : (s + 1) * HALF // 16]),
+            )
 
         def group_wa(a, t0, name, on_vector=False):
             pair = held([P, 2, P, PACK], BF16, name)
@@ -162,11 +155,12 @@ def tile_list_tenant_adapter_queries_kernel(
                 nc.scalar.activation(out=dst, in_=src, func=COPY)
             return pair
 
-        def quantize_wa(a, t0, pair):
+        def quantize_wa(a, t0, pair, first=0, count=2):
+            cols = slice((t0 + first) * P, (t0 + first + count) * P)
             nc.vector.quantize_mx(
-                out=wa_q[a][:, t0 * P : (t0 + 2) * P].bitcast(FP8X4),
-                scales=wa_sc[a][:, t0 * P : (t0 + 2) * P],
-                in_=pair[:].rearrange("p t m j -> p (t m j)"),
+                out=wa_q[a][:, cols].bitcast(FP8X4),
+                scales=wa_sc[a][:, cols],
+                in_=pair[:, first : first + count].rearrange("p t m j -> p (t m j)"),
             )
 
         def down(acc, a, s, t, start, stop):
@@ -180,26 +174,24 @@ def tile_list_tenant_adapter_queries_kernel(
                 stop=stop,
             )
 
-        def dense(acc, a, s, n):
+        def dense(acc, a, s, n, lo=0, hi=HALF):
             part, col = (0, n * P) if n * P < EARLY_N else (1, n * P - EARLY_N)
-            cols = slice(s * HALF, (s + 1) * HALF)
             nc.tensor.matmul_mx(
-                out=acc[:],
+                out=acc[:, : hi - lo],
                 lhsT=wd[part][:, a, 2 * col : 2 * (col + P)].bitcast(FP4X4),
                 lhsT_scale=wd_sc[part][:, a, col : col + P],
-                rhs=v[a, s].bitcast(FP8X4),
-                rhs_scale=v_sc[:, a, cols],
+                rhs=v[a, s][:, lo:hi].bitcast(FP8X4),
+                rhs_scale=v_sc[:, a, s * HALF + lo : s * HALF + hi],
                 start=(a == 0),
                 stop=False,
             )
 
-        first = [[bank(PACK * s + t) for t in range(PACK)] for s in range(HALVES)]
-        slots = (2, 3, 0, 1)
+        first = [[bank(PACK * s + t) for t in range(PACK)] for s in range(2)]
         gather_both(0)
         quantize_wa(0, 0, group_wa(0, 0, "v1"))
         quantize_wa(0, 2, group_wa(0, 2, "wa_pair0_2"))
         for t in range(PACK):
-            for s in range(HALVES):
+            for s in range(2):
                 down(first[s][t], 0, s, t, True, False)
         gather_both(1)
         low = group_wa(1, 0, "wa_pair1_0")
@@ -208,48 +200,53 @@ def tile_list_tenant_adapter_queries_kernel(
         load_wd(1)
         wd_sc.append(held([P, PASSES, N - EARLY_N], U8, "wa_raw1", later))
         clear(wd_sc[1][:].rearrange("p a n -> p (a n)").bitcast(I32))
-        load_wd_scales(1, nc.sync)
-        load_gain(0)
-        load_wb(0)
-        load_gain(1)
-        load_wb(1)
-        for t in slots:
+        load_wd_scales(1)
+        nc.sync.dma_start(out=gains[0][:], in_=rows_by_four(gain, *gain_cols[0]))
+        for part in range(2):
+            nc.sync.dma_start(out=wb_raw[part][:], in_=rows_by_four(wb, *wb_cols[part]))
+        for part in (1, 2):
+            nc.sync.dma_start(out=gains[part][:], in_=rows_by_four(gain, *gain_cols[part]))
+        for t in SLOTS:
             down(first[1][t], 1, 1, t, False, True)
-        for t in slots:
+        for t in SLOTS:
             down(first[0][t], 1, 0, t, False, False)
         h_part = held([P, PACK, HALF], F32, "h_part")
-        for t in slots:
+        for t in SLOTS:
             nc.scalar.activation(out=h_part[:, t, :], in_=first[1][t][:], func=COPY)
 
         accs = {}
-        early = [(s, n) for s in range(HALVES) for n in range(EARLY_N // P)]
+        early = [(s, n) for s in range(2) for n in range(EARLY_N // P)]
         for i, tile in enumerate(early):
-            accs[tile] = bank(PACK + slots[i])
+            accs[tile] = bank(PACK + SLOTS[i])
             for a in range(2):
                 dense(accs[tile], a, *tile)
         gather_both(2)
         for tile in early:
             dense(accs[tile], 2, *tile)
-        for s in range(HALVES):
-            gather(3, s)
+        for s in range(2):
+            gather_half(3, s)
         for tile in early:
             dense(accs[tile], 3, *tile)
-        for a in (2, 3):
-            low = group_wa(a, 0, "wa_pair%d_0" % a)
-            quantize_wa(a, 2, group_wa(a, 2, "wa_pair%d_2" % a, True))
-            quantize_wa(a, 0, low)
-            if a == 2:
-                for t in slots:
-                    down(first[0][t], 2, 0, t, False, False)
+        low = group_wa(2, 0, "wa_pair2_0")
+        quantize_wa(2, 2, group_wa(2, 2, "wa_pair2_2", True))
+        quantize_wa(2, 0, low)
+        for t in SLOTS:
+            down(first[0][t], 2, 0, t, False, False)
+        low = group_wa(3, 0, "wa_pair3_0")
+        high = group_wa(3, 2, "wa_pair3_2", True)
+        for i in range(2):
+            quantize_wa(3, 2, high, i, 1)
+        quantize_wa(3, 0, low)
         bias = held([P, 256], F32, "wa_pair3_0")
         nc.vector.transpose(bias[:], bias_rows[:])
+
         h_both = held([P, PACK + 2, HALF], F32, "h_both")
         h_sum = [h_both[:, 0:PACK, :], h_both[:, 2:, :]]
-        for t in slots:
+        for t in SLOTS:
             down(first[0][t], 3, 0, t, False, True)
             nc.scalar.activation(out=h_sum[0][:, t, :], in_=first[0][t][:], func=COPY)
         h_rest = held([P, 2, HALF], F32, "h_rest")
-        for t in slots:
+        for t in SLOTS:
             second = bank(t)
             down(second, 2, 1, t, True, False)
             down(second, 3, 1, t, False, True)
@@ -263,90 +260,92 @@ def tile_list_tenant_adapter_queries_kernel(
             for a in range(PASSES):
                 dense(accs[tile], a, *tile)
 
-        for i, t in enumerate(slots):
+        for i, t in enumerate(SLOTS):
             open_tile((0, EARLY_N // P + i), t)
 
-        def by_fours(ap, form):
-            return ap.rearrange(form + " -> p c t i", i=PACK)
-
-        h_grouped = []
-        h_q = [held([P, HALF], U32, "h_q%d" % s) for s in range(HALVES)]
-        h_sc = [held([P, HALF], U8, "h_sc%d" % s) for s in range(HALVES)]
-        wb_q = []
+        h_q = [held([P, HALF], U32, "h_q%d" % s) for s in range(2)]
+        h_sc = [held([P, HALF], U8, "h_sc%d" % s) for s in range(2)]
+        wb_q = [held([P, WB_PART], U32, "wb_q%d" % part) for part in range(N // WB_PART)]
         wb_sc = held([P, N], U8, "wb_sc")
 
-        def weigh_h(s):
-            h_grouped.append(held([P, HALF, PACK], BF16, "h_grouped%d" % s))
+        def weigh_h(part, name):
+            lo, hi = gain_cols[part]
+            grouped = held([P, hi - lo, PACK], BF16, name)
             nc.vector.tensor_tensor(
-                out=by_fours(h_grouped[s][:], "p (c i) t"),
-                in0=by_fours(h_sum[s], "p t (c i)"),
-                in1=by_fours(gains[s][:], "p t (c i)"),
+                out=by_fours(grouped[:], "p (c i) t"),
+                in0=by_fours(h_sum[lo // HALF][:, :, lo % HALF : lo % HALF + hi - lo], "p t (c i)"),
+                in1=by_fours(gains[part][:], "p t (c i)"),
                 op=MULT,
             )
+            return grouped
 
-        def quantize_h(s):
+        def quantize_h(part, grouped):
+            lo, hi = gain_cols[part]
+            cols = slice(lo % HALF, lo % HALF + hi - lo)
             nc.vector.quantize_mx(
-                out=h_q[s][:].bitcast(FP8X4), scales=h_sc[s][:], in_=h_grouped[s][:].rearrange("p s t -> p (s t)")
+                out=h_q[lo // HALF][:, cols].bitcast(FP8X4),
+                scales=h_sc[lo // HALF][:, cols],
+                in_=grouped[:].rearrange("p s t -> p (s t)"),
             )
 
-        def quantize_wb(part):
+        def group_wb(part, name):
             lo = part * WB_PART
             raw, col = (wb_raw[0], lo) if lo + WB_PART < N else (wb_raw[1], 0)
-            wb_grouped = held([P, WB_PART, PACK], BF16, "h_grouped1" if part == 1 else "wb_grouped%d" % part)
+            grouped = held([P, WB_PART, PACK], BF16, name)
             nc.scalar.activation(
-                out=by_fours(wb_grouped[:], "p (c i) t"),
+                out=by_fours(grouped[:], "p (c i) t"),
                 in_=by_fours(raw[:, :, col : col + WB_PART], "p t (c i)"),
                 func=COPY,
             )
-            wb_q.append(held([P, WB_PART], U32, "h_grouped1" if part == 2 else "wb_q%d" % part))
+            return grouped
+
+        def quantize_wb(part, grouped):
             nc.vector.quantize_mx(
                 out=wb_q[part][:].bitcast(FP8X4),
-                scales=wb_sc[:, lo : lo + WB_PART],
-                in_=wb_grouped[:].rearrange("p n j -> p (n j)"),
+                scales=wb_sc[:, part * WB_PART : (part + 1) * WB_PART],
+                in_=grouped[:].rearrange("p n j -> p (n j)"),
             )
 
-        weigh_h(0)
-        quantize_h(0)
+        grouped = weigh_h(0, "h_grouped0")
         nc.vector.tensor_tensor(out=h_sum[1][:, :2, :], in0=h_rest[:], in1=h_part[:, :2, :], op=ADD)
-        quantize_wb(0)
-        quantize_wb(1)
-        weigh_h(1)
-        quantize_h(1)
-        quantize_wb(2)
+        quantize_h(0, grouped)
+        wb_grouped = [group_wb(part, "wb_grouped%d" % part) for part in range(3)]
+        quantize_wb(0, wb_grouped[0])
+        quantize_wb(1, wb_grouped[1])
+        third = weigh_h(1, "wb_grouped1")
+        quantize_wb(2, wb_grouped[2])
+        fourth = weigh_h(2, "wb_grouped2")
+        quantize_h(1, third)
+        quantize_h(2, fourth)
 
-        def finish(s, n):
-            acc = accs[s, n]
+        def finish(acc, s, n, on_vector, lo=0, hi=HALF):
             nc.tensor.matmul_mx(
-                out=acc[:],
+                out=acc[:, : hi - lo],
                 lhsT=wb_q[n // 2][:, n % 2 * P : (n % 2 + 1) * P].bitcast(FP8X4),
                 lhsT_scale=wb_sc[:, n * P : (n + 1) * P],
-                rhs=h_q[s][:].bitcast(FP8X4),
-                rhs_scale=h_sc[s][:],
+                rhs=h_q[s][:, lo:hi].bitcast(FP8X4),
+                rhs_scale=h_sc[s][:, lo:hi],
                 start=False,
                 stop=True,
             )
-            pieces = 2 if (s, n) == (HALVES - 1, N_TILES - 1) else 1
-            width = HALF // pieces
-            for i in range(pieces):
-                result = stage.tile([P, width], F32, name="result")
-                sums = acc[:, i * width : (i + 1) * width]
-                if s == 0 and n >= 4:
-                    nc.vector.tensor_scalar(
-                        out=result[:], in0=sums, scalar1=bias[:, 32 * n : 32 * n + 1], scalar2=None, op0=ADD
-                    )
-                else:
-                    nc.scalar.activation(out=result[:], in_=sums, func=IDENTITY, bias=bias[:, 32 * n : 32 * n + 1])
-                col = s * HALF + i * width
-                nc.sync.dma_start(out=out[n * P : (n + 1) * P, col : col + width], in_=result[:])
+            result = stage.tile([P, hi - lo], F32, name="result")
+            column = bias[:, 32 * n : 32 * n + 1]
+            if on_vector:
+                nc.vector.tensor_scalar(out=result[:], in0=acc[:, : hi - lo], scalar1=column, scalar2=None, op0=ADD)
+            else:
+                nc.scalar.activation(out=result[:], in_=acc[:, : hi - lo], func=IDENTITY, bias=column)
+            nc.sync.dma_start(out=out[n * P : (n + 1) * P, s * HALF + lo : s * HALF + hi], in_=result[:])
 
-        for n in range(4):
-            finish(0, n)
+        for n in range(N_TILES):
+            finish(accs[0, n], 0, n, False)
         open_tile((1, 2), 6)
         open_tile((1, 3), 7)
         for n in range(4):
-            finish(1, n)
-        finish(0, 4)
-        finish(0, 5)
-        for n, b in ((4, 4), (5, 5)):
-            open_tile((1, n), b)
-            finish(1, n)
+            finish(accs[1, n], 1, n, n % 2 == 0)
+        open_tile((1, 4), 2)
+        finish(accs[1, 4], 1, 4, False)
+        for b, lo in ((4, 0), (5, QUARTER)):
+            acc = bank(b)
+            for a in range(PASSES):
+                dense(acc, a, 1, 5, lo, lo + QUARTER)
+            finish(acc, 1, 5, lo == 0, lo, lo + QUARTER)

@@ -61,7 +61,6 @@ def tile_list_tenant_adapter_queries_kernel(
         wa_raw = [held([P, PACK, R], F32, "wa_raw0")]
         tab = [held([P, T], I32, "tab%d" % a) for a in range(2)]
         wd_cols = ((0, EARLY_N), (EARLY_N, N))
-        wb_cols = ((0, 2 * WB_PART), (2 * WB_PART, N))
         gain_cols = ((0, HALF), (HALF, HALF + QUARTER), (HALF + QUARTER, S))
 
         def load_wa(a):
@@ -106,7 +105,7 @@ def tile_list_tenant_adapter_queries_kernel(
         wd = [held([P, PASSES, 2 * (hi - lo)], U8, "wd%d" % lo, later) for lo, hi in wd_cols]
         wd_sc = [held([P, PASSES, EARLY_N], U8, "wd_sc0", later)]
         gains = [held([P, PACK, hi - lo], F32, "gain%d" % lo, later) for lo, hi in gain_cols]
-        wb_raw = [held([P, PACK, hi - lo], F32, "wb_raw%d" % lo, later) for lo, hi in wb_cols]
+        wb_raw = [held([P, PACK, WB_PART], F32, "wb_raw%d" % part, later) for part in range(N // WB_PART)]
         bias_rows = held([P, 256], F32, "bias_rows", later)
 
         for q in (0, 2, 1, 3):
@@ -202,8 +201,8 @@ def tile_list_tenant_adapter_queries_kernel(
         clear(wd_sc[1][:].rearrange("p a n -> p (a n)").bitcast(I32))
         load_wd_scales(1)
         nc.sync.dma_start(out=gains[0][:], in_=rows_by_four(gain, *gain_cols[0]))
-        for part in range(2):
-            nc.sync.dma_start(out=wb_raw[part][:], in_=rows_by_four(wb, *wb_cols[part]))
+        for part in range(N // WB_PART):
+            nc.sync.dma_start(out=wb_raw[part][:], in_=rows_by_four(wb, part * WB_PART, (part + 1) * WB_PART))
         for part in (1, 2):
             nc.sync.dma_start(out=gains[part][:], in_=rows_by_four(gain, *gain_cols[part]))
         for t in SLOTS:
@@ -236,7 +235,8 @@ def tile_list_tenant_adapter_queries_kernel(
         high = group_wa(3, 2, "wa_pair3_2", True)
         for i in range(2):
             quantize_wa(3, 2, high, i, 1)
-        quantize_wa(3, 0, low)
+        for i in range(2):
+            quantize_wa(3, 0, low, i, 1)
         bias = held([P, 256], F32, "wa_pair3_0")
         nc.vector.transpose(bias[:], bias_rows[:])
 
@@ -289,12 +289,10 @@ def tile_list_tenant_adapter_queries_kernel(
             )
 
         def group_wb(part, name):
-            lo = part * WB_PART
-            raw, col = (wb_raw[0], lo) if lo + WB_PART < N else (wb_raw[1], 0)
             grouped = held([P, WB_PART, PACK], BF16, name)
             nc.scalar.activation(
                 out=by_fours(grouped[:], "p (c i) t"),
-                in_=by_fours(raw[:, :, col : col + WB_PART], "p t (c i)"),
+                in_=by_fours(wb_raw[part][:], "p t (c i)"),
                 func=COPY,
             )
             return grouped
@@ -310,11 +308,10 @@ def tile_list_tenant_adapter_queries_kernel(
         nc.vector.tensor_tensor(out=h_sum[1][:, :2, :], in0=h_rest[:], in1=h_part[:, :2, :], op=ADD)
         quantize_h(0, grouped)
         wb_grouped = [group_wb(part, "wb_grouped%d" % part) for part in range(3)]
-        quantize_wb(0, wb_grouped[0])
-        quantize_wb(1, wb_grouped[1])
-        third = weigh_h(1, "wb_grouped1")
-        quantize_wb(2, wb_grouped[2])
-        fourth = weigh_h(2, "wb_grouped2")
+        for part in range(3):
+            quantize_wb(part, wb_grouped[part])
+        third = weigh_h(1, "wb_grouped2")
+        fourth = weigh_h(2, "wb_grouped1")
         quantize_h(1, third)
         quantize_h(2, fourth)
 

from contextlib import ExitStack

import concourse.mybir as mybir

K, R, N, T, S = 2048, 512, 768, 2048, 1024
FLOPS = 2 * S * (K * R + K * N + R * N)

F32 = mybir.dt.float32
BF16 = mybir.dt.bfloat16
I32 = mybir.dt.int32
U32 = mybir.dt.uint32
U16 = mybir.dt.uint16
U8 = mybir.dt.uint8
FP8X4 = mybir.dt.float8_e4m3fn_x4
FP4X4 = mybir.dt.float4_e2m1fn_x4
COPY = mybir.ActivationFunctionType.Copy
IDENTITY = mybir.ActivationFunctionType.Identity
MULT = mybir.AluOpType.mult
ADD = mybir.AluOpType.add

P = 128
PACK = 4
PASSES = K // (P * PACK)
HALF = 512
QUARTER = 256
N_TILES = N // P
QUADS = 4
SCALE_ROW0 = 32
WB_PART = 256
EARLY_N = 256
SLOTS = (2, 3, 0, 1)


def tile_list_tenant_adapter_queries_kernel(
    tc, tab_words, tab_scales, offs, wd_words, wd_scales, wa, wb, gain, bq, out
):
    nc = tc.nc
    with ExitStack() as ctx:
        keep = ctx.enter_context(tc.tile_pool(name="keep", bufs=1))
        stage = ctx.enter_context(tc.tile_pool(name="stage", bufs=13))
        psum = ctx.enter_context(tc.psum_pool(name="psum", bufs=1))

        def held(shape, dtype, name, pool=keep):
            return pool.tile(shape, dtype, name=name, align_bytes=64)

        def bank(b):
            return psum.tile([P, HALF], F32, name="bank%d" % b)

        def clear(words):
            nc.vector.memset(words, 0)

        def rows_by_four(x, lo, hi):
            return x[:, lo:hi].rearrange("(p j) c -> p j c", j=PACK)

        def by_fours(ap, form):
            return ap.rearrange(form + " -> p c t i", i=PACK)

        offsets = keep.tile([P, S // 16], U16, name="offsets")
        v_rows = held([P, S], U8, "v_rows")
        v_sc = held([P, PASSES, S], U8, "v_sc")
        wa_raw = [held([P, PACK, R], F32, "wa_raw0")]
        tab = [held([P, T], I32, "tab%d" % a) for a in range(2)]
        wd_cols = ((0, EARLY_N), (EARLY_N, N))
        gain_cols = ((0, HALF), (HALF, HALF + QUARTER), (HALF + QUARTER, S))

        def load_wa(a):
            nc.sync.dma_start(out=wa_raw[a][:], in_=rows_by_four(wa[a * P * PACK : (a + 1) * P * PACK, :], 0, R))

        def load_tab(a):
            nc.sync.dma_start(out=tab[a][:], in_=tab_words[a].rearrange("p t i -> p (t i)").bitcast(I32))

        def load_wd_scales(part):
            lo, hi = wd_cols[part]
            for r in range(4):
                nc.sync.dma_start(
                    out=wd_sc[part][r:P:32, :, :].bitcast(I32),
                    in_=wd_scales[:, r:16:4, lo:hi].rearrange("a q n -> q a n").bitcast(I32),
                )

        def load_wd(part):
            lo, hi = wd_cols[part]
            nc.sync.dma_start(
                out=wd[part][:].bitcast(I32),
                in_=wd_words[:, :, 2 * lo : 2 * hi].rearrange("a p c -> p a c").bitcast(I32),
            )

        with tc.tile_pool(name="window", bufs=1) as window:
            tab_sc = held([P, T], U8, "tab_sc", window)
            nc.sync.dma_start(offsets[:], offs)
            nc.sync.dma_start(
                out=tab_sc[SCALE_ROW0 : SCALE_ROW0 + 64, :].bitcast(I32),
                in_=tab_scales.rearrange("a s t -> s a t").bitcast(I32),
            )
            load_tab(0)
            load_wa(0)
            load_tab(1)
            clear(tab_sc[:SCALE_ROW0, :].bitcast(I32))
            clear(tab_sc[SCALE_ROW0 + 64 :, :].bitcast(I32))
            clear(v_sc[:].rearrange("p a s -> p (a s)").bitcast(I32))
            nc.vector.tensor_copy(out=v_rows[:], in_=tab_sc[:].indirect(offsets[:]))

        later = ctx.enter_context(tc.tile_pool(name="later", bufs=1))
        wa_raw.extend(held([P, PACK, R], F32, "wa_raw%d" % a, later) for a in range(1, PASSES))
        tab.extend(held([P, T], I32, "tab%d" % a, later) for a in range(2, PASSES))
        wd = [held([P, PASSES, 2 * (hi - lo)], U8, "wd%d" % lo, later) for lo, hi in wd_cols]
        wd_sc = [held([P, PASSES, EARLY_N], U8, "wd_sc0", later)]
        gains = [held([P, PACK, hi - lo], F32, "gain%d" % lo, later) for lo, hi in gain_cols]
        wb_raw = [held([P, PACK, WB_PART], F32, "wb_raw%d" % part, later) for part in range(N // WB_PART)]
        bias_rows = held([P, 256], F32, "bias_rows", later)

        for q in (0, 2, 1, 3):
            nc.sync.dma_start(
                out=v_sc[32 * q : 32 * q + 4, :, :].bitcast(I32),
                in_=v_rows[SCALE_ROW0 + 16 * q : SCALE_ROW0 + 16 * (q + 1), :].bitcast(I32),
            )
        load_wa(1)
        load_tab(2)
        clear(wd_sc[0][:].rearrange("p a n -> p (a n)").bitcast(I32))
        clear(bias_rows[:].bitcast(I32))
        load_wd_scales(0)
        load_wd(0)
        load_tab(3)
        load_wa(2)
        load_wa(3)
        nc.sync.dma_start(
            out=bias_rows[0:P:32, 0 : 32 * N_TILES].rearrange("q (c i) -> q c i", i=32),
            in_=bq.rearrange("(c q i) -> q c i", q=QUADS, i=32),
        )

        v = {}
        wa_q = [held([P, R], U32, "wa_q%d" % a) for a in range(PASSES)]
        wa_sc = [held([P, R], U8, "wa_sc%d" % a) for a in range(PASSES)]

        def gather_both(a):
            both = held([P, S], U32, "v%d" % a)
            nc.vector.tensor_copy(out=both[:], in_=tab[a][:].bitcast(U32).indirect(offsets[:]))
            for s in range(2):
                v[a, s] = both[:, s * HALF : (s + 1) * HALF]

        def gather_half(a, s):
            v[a, s] = held([P, HALF], U32, "v%d_%d" % (a, s))[:]
            nc.vector.tensor_copy(
                out=v[a, s],
                in_=tab[a][:].bitcast(U32).indirect(offsets[:, s * HALF // 16 : (s + 1) * HALF // 16]),
            )

        def group_wa(a, t0, name, on_vector=False):
            pair = held([P, 2, P, PACK], BF16, name)
            dst = pair[:].rearrange("p t m j -> p m j t")
            src = wa_raw[a][:].rearrange("p j (m t) -> p m j t", t=PACK)[:, :, :, t0 : t0 + 2]
            if on_vector:
                nc.vector.tensor_copy(out=dst, in_=src)
            else:
                nc.scalar.activation(out=dst, in_=src, func=COPY)
            return pair

        def quantize_wa(a, t0, pair, first=0, count=2):
            cols = slice((t0 + first) * P, (t0 + first + count) * P)
            nc.vector.quantize_mx(
                out=wa_q[a][:, cols].bitcast(FP8X4),
                scales=wa_sc[a][:, cols],
                in_=pair[:, first : first + count].rearrange("p t m j -> p (t m j)"),
            )

        def down(acc, a, s, t, start, stop):
            nc.tensor.matmul_mx(
                out=acc[:],
                lhsT=wa_q[a][:, t * P : (t + 1) * P].bitcast(FP8X4),
                lhsT_scale=wa_sc[a][:, t * P : (t + 1) * P],
                rhs=v[a, s].bitcast(FP8X4),
                rhs_scale=v_sc[:, a, s * HALF : (s + 1) * HALF],
                start=start,
                stop=stop,
            )

        def dense(acc, a, s, n, lo=0, hi=HALF):
            part, col = (0, n * P) if n * P < EARLY_N else (1, n * P - EARLY_N)
            nc.tensor.matmul_mx(
                out=acc[:, : hi - lo],
                lhsT=wd[part][:, a, 2 * col : 2 * (col + P)].bitcast(FP4X4),
                lhsT_scale=wd_sc[part][:, a, col : col + P],
                rhs=v[a, s][:, lo:hi].bitcast(FP8X4),
                rhs_scale=v_sc[:, a, s * HALF + lo : s * HALF + hi],
                start=(a == 0),
                stop=False,
            )

        first = [[bank(PACK * s + t) for t in range(PACK)] for s in range(2)]
        gather_both(0)
        quantize_wa(0, 0, group_wa(0, 0, "v1"))
        quantize_wa(0, 2, group_wa(0, 2, "wa_pair0_2"))
        for t in range(PACK):
            for s in range(2):
                down(first[s][t], 0, s, t, True, False)
        gather_both(1)
        low = group_wa(1, 0, "wa_pair1_0")
        quantize_wa(1, 2, group_wa(1, 2, "wa_pair1_2", True))
        quantize_wa(1, 0, low)
        load_wd(1)
        wd_sc.append(held([P, PASSES, N - EARLY_N], U8, "wa_raw1", later))
        clear(wd_sc[1][:].rearrange("p a n -> p (a n)").bitcast(I32))
        load_wd_scales(1)
        nc.sync.dma_start(out=gains[0][:], in_=rows_by_four(gain, *gain_cols[0]))
        for part in range(N // WB_PART):
            nc.sync.dma_start(out=wb_raw[part][:], in_=rows_by_four(wb, part * WB_PART, (part + 1) * WB_PART))
        for part in (1, 2):
            nc.sync.dma_start(out=gains[part][:], in_=rows_by_four(gain, *gain_cols[part]))
        for t in SLOTS:
            down(first[1][t], 1, 1, t, False, True)
        for t in SLOTS:
            down(first[0][t], 1, 0, t, False, False)
        h_part = held([P, PACK, HALF], F32, "h_part")
        for t in SLOTS:
            nc.scalar.activation(out=h_part[:, t, :], in_=first[1][t][:], func=COPY)

        accs = {}
        early = [(s, n) for s in range(2) for n in range(EARLY_N // P)]
        for i, tile in enumerate(early):
            accs[tile] = bank(PACK + SLOTS[i])
            for a in range(2):
                dense(accs[tile], a, *tile)
        gather_both(2)
        for tile in early:
            dense(accs[tile], 2, *tile)
        for s in range(2):
            gather_half(3, s)
        for tile in early:
            dense(accs[tile], 3, *tile)
        low = group_wa(2, 0, "wa_pair2_0")
        quantize_wa(2, 2, group_wa(2, 2, "wa_pair2_2", True))
        quantize_wa(2, 0, low)
        for t in SLOTS:
            down(first[0][t], 2, 0, t, False, False)
        low = group_wa(3, 0, "wa_pair3_0")
        high = group_wa(3, 2, "wa_pair3_2", True)
        for i in range(2):
            quantize_wa(3, 2, high, i, 1)
        for i in range(2):
            quantize_wa(3, 0, low, i, 1)
        bias = held([P, 256], F32, "wa_pair3_0")
        nc.vector.transpose(bias[:], bias_rows[:])

        h_both = held([P, PACK + 2, HALF], F32, "h_both")
        h_sum = [h_both[:, 0:PACK, :], h_both[:, 2:, :]]
        for t in SLOTS:
            down(first[0][t], 3, 0, t, False, True)
            nc.scalar.activation(out=h_sum[0][:, t, :], in_=first[0][t][:], func=COPY)
        h_rest = held([P, 2, HALF], F32, "h_rest")
        for t in SLOTS:
            second = bank(t)
            down(second, 2, 1, t, True, False)
            down(second, 3, 1, t, False, True)
            if t >= 2:
                nc.vector.tensor_tensor(out=h_sum[1][:, t, :], in0=second[:], in1=h_part[:, t, :], op=ADD)
            else:
                nc.scalar.activation(out=h_rest[:, t, :], in_=second[:], func=COPY)

        def open_tile(tile, b):
            accs[tile] = bank(b)
            for a in range(PASSES):
                dense(accs[tile], a, *tile)

        for i, t in enumerate(SLOTS):
            open_tile((0, EARLY_N // P + i), t)

        h_q = [held([P, HALF], U32, "h_q%d" % s) for s in range(2)]
        h_sc = [held([P, HALF], U8, "h_sc%d" % s) for s in range(2)]
        wb_q = [held([P, WB_PART], U32, "wb_q%d" % part) for part in range(N // WB_PART)]
        wb_sc = held([P, N], U8, "wb_sc")

        def weigh_h(part, name):
            lo, hi = gain_cols[part]
            grouped = held([P, hi - lo, PACK], BF16, name)
            nc.vector.tensor_tensor(
                out=by_fours(grouped[:], "p (c i) t"),
                in0=by_fours(h_sum[lo // HALF][:, :, lo % HALF : lo % HALF + hi - lo], "p t (c i)"),
                in1=by_fours(gains[part][:], "p t (c i)"),
                op=MULT,
            )
            return grouped

        def quantize_h(part, grouped):
            lo, hi = gain_cols[part]
            cols = slice(lo % HALF, lo % HALF + hi - lo)
            nc.vector.quantize_mx(
                out=h_q[lo // HALF][:, cols].bitcast(FP8X4),
                scales=h_sc[lo // HALF][:, cols],
                in_=grouped[:].rearrange("p s t -> p (s t)"),
            )

        def group_wb(part, name):
            grouped = held([P, WB_PART, PACK], BF16, name)
            nc.scalar.activation(
                out=by_fours(grouped[:], "p (c i) t"),
                in_=by_fours(wb_raw[part][:], "p t (c i)"),
                func=COPY,
            )
            return grouped

        def quantize_wb(part, grouped):
            nc.vector.quantize_mx(
                out=wb_q[part][:].bitcast(FP8X4),
                scales=wb_sc[:, part * WB_PART : (part + 1) * WB_PART],
                in_=grouped[:].rearrange("p n j -> p (n j)"),
            )

        grouped = weigh_h(0, "h_grouped0")
        nc.vector.tensor_tensor(out=h_sum[1][:, :2, :], in0=h_rest[:], in1=h_part[:, :2, :], op=ADD)
        quantize_h(0, grouped)
        wb_grouped = [group_wb(part, "wb_grouped%d" % part) for part in range(3)]
        for part in range(3):
            quantize_wb(part, wb_grouped[part])
        third = weigh_h(1, "wb_grouped2")
        fourth = weigh_h(2, "wb_grouped1")
        quantize_h(1, third)
        quantize_h(2, fourth)

        def finish(acc, s, n, on_vector, lo=0, hi=HALF):
            nc.tensor.matmul_mx(
                out=acc[:, : hi - lo],
                lhsT=wb_q[n // 2][:, n % 2 * P : (n % 2 + 1) * P].bitcast(FP8X4),
                lhsT_scale=wb_sc[:, n * P : (n + 1) * P],
                rhs=h_q[s][:, lo:hi].bitcast(FP8X4),
                rhs_scale=h_sc[s][:, lo:hi],
                start=False,
                stop=True,
            )
            result = stage.tile([P, hi - lo], F32, name="result")
            column = bias[:, 32 * n : 32 * n + 1]
            if on_vector:
                nc.vector.tensor_scalar(out=result[:], in0=acc[:, : hi - lo], scalar1=column, scalar2=None, op0=ADD)
            else:
                nc.scalar.activation(out=result[:], in_=acc[:, : hi - lo], func=IDENTITY, bias=column)
            nc.sync.dma_start(out=out[n * P : (n + 1) * P, s * HALF + lo : s * HALF + hi], in_=result[:])

        for n in range(N_TILES):
            finish(accs[0, n], 0, n, False)
        open_tile((1, 2), 6)
        open_tile((1, 3), 7)
        for n in range(4):
            finish(accs[1, n], 1, n, n % 2 == 0)
        open_tile((1, 4), 2)
        finish(accs[1, 4], 1, 4, False)
        for b, lo in ((4, 0), (5, QUARTER)):
            acc = bank(b)
            for a in range(PASSES):
                dense(acc, a, 1, 5, lo, lo + QUARTER)
            finish(acc, 1, 5, lo == 0, lo, lo + QUARTER)
